import numpy as np
CORES = [21,29,37,45,53,61,69,77,85]
N = 9
T, G, CAP = 4096, 4096, 512
def entries(a): return a.T.reshape(-1)
def pack(v, P): return np.ascontiguousarray(np.asarray(v, np.int32).reshape(-1, P).T)
def lists(rng, how):
    S = rng.integers(0, T, (N, 2 * CAP)); P = np.stack([rng.permutation(G)[:2 * CAP] for r in range(N)])
    if how == "alike": S[:] = rng.integers(0, T, (N, 1))
    if how == "edge":
        S = np.where(rng.random((N, 2 * CAP)) < 0.5, 0, T - 1); S[:, [0, CAP]] = 0; S[:, [1, CAP + 1]] = T - 1
        P[:, 1:-1] = np.stack([1 + rng.permutation(G - 2)[:2 * CAP - 2] for r in range(N)]); P[0::2, 0], P[0::2, -1] = 0, G - 1; P[1::2, 0], P[1::2, -1] = G - 1, 0
    if how == "mixed": P = np.stack([rng.permutation(2 * CAP) for r in range(N)]); P[1::2] += G - 2 * CAP
    if how == "sorted":
        S2, P2 = [-np.sort(-A.reshape(N, 2, CAP), axis=2).reshape(N, 2 * CAP) for A in (S, P)]; S, P = -np.sort(-S, axis=1), -np.sort(-P, axis=1)
        S[1::3], P[1::3] = S[1::3, ::-1].copy(), P[1::3, ::-1].copy(); S[2::3], P[2::3] = S2[2::3], P2[2::3]
    return {"snd": np.stack([pack(s, 16) for s in S]), "plc": np.stack([pack(q, 16) for q in P])}
def setup_inputs(rng):
    return dict({"x": rng.standard_normal((N, 128, T), dtype=np.float32), "gh": rng.standard_normal((N, 128, G), dtype=np.float32)}, **lists(rng, "uniform"))
def setup_inputs_alike(rng):
    d = setup_inputs(rng); d.update(lists(rng, "alike"))
    for k in ("x", "gh"): d[k] = (d[k].astype(np.float32) * 1048576.0).astype(d[k].dtype)
    return d
def setup_inputs_edge(rng):
    d = setup_inputs(rng); d.update(lists(rng, "edge"))
    for k in ("x", "gh"): d[k] = (d[k].astype(np.float32) * (1 / 1024.0)).astype(d[k].dtype)
    return d
def setup_inputs_mixed(rng):
    d = setup_inputs(rng); d.update(lists(rng, "mixed"))
    return d
def setup_inputs_sorted(rng):
    d = setup_inputs(rng); d.update(lists(rng, "sorted"))
    return d
def setup_inputs_zeros(rng):
    d = setup_inputs(rng); d.update(lists(rng, "zeros"))
    for r in range(N): d["x"][r][:, entries(d["snd"][r])[::2]] = 0
    return d
def check_inputs(x):
    bad = []
    if x["snd"].min() < 0 or x["snd"].max() >= T: bad.append("snd out of range")
    if x["plc"].min() < 0 or x["plc"].max() >= G: bad.append("plc out of range")
    if any(len(np.unique(a)) != a.size for a in x["plc"]): bad.append("a place is named twice")
    return bad
def reference(x, gh, snd, plc):
    y = gh.copy()
    for r in range(N):
        S = entries(snd[r]); lo, hi = (r - 1) % N, (r + 1) % N
        y[lo][:, entries(plc[lo])[CAP:]] = x[r][:, S[:CAP]]
        y[hi][:, entries(plc[hi])[:CAP]] = x[r][:, S[CAP:]]
    return {"y": y}

@@ -1,0 +1,222 @@
+from concourse.bass import DstId, RemoteDMATransfer
+from concourse.mybir import AluOpType, ActivationFunctionType
+
+SIM = 96
+W, CAP, HALF = 4096, 512, 256
+NB = 8
+BLOCKS = (640, 1216, 2240)
+
+SCRATCH = {
+    "xs": ("sbuf", [128, W], "float32"),
+    "tab": ("sbuf", [128, W + 2 * CAP], "float32"),
+    "ys": ("sbuf", [128, W], "float32"),
+    "outb": ("sbuf", [128, 2 * CAP], "float32"),
+    "relay": ("sbuf", [128, HALF], "float32"),
+    "sndi": ("sbuf", [128, 64], "int32"),
+    "sndf": ("sbuf", [128, 64], "float32"),
+    "ofs": ("sbuf", [128, 64], "uint16"),
+    "plci": ("sbuf", [128, NB], "int32"),
+    "plcf": ("sbuf", [128, NB], "float32"),
+    "phi": ("sbuf", [128, NB], "int32"),
+    "pli": ("sbuf", [128, NB], "int32"),
+    "phf": ("sbuf", [128, NB], "float32"),
+    "plf": ("sbuf", [128, NB], "float32"),
+    "val": ("sbuf", [128, NB], "float32"),
+    "ib": ("sbuf", [128, NB], "float32"),
+    "iv": ("sbuf", [128, NB], "float32"),
+    "pidx": ("sbuf", [128, 1], "int32"),
+    "mi": ("sbuf", [128, 1], "int32"),
+    "qi": ("sbuf", [128, 1], "int32"),
+    "pf": ("sbuf", [128, 1], "float32"),
+    "mf": ("sbuf", [128, 1], "float32"),
+    "qf": ("sbuf", [128, 1], "float32"),
+    "qrow": ("sbuf", [128, 128], "float32"),
+    "rr": ("sbuf", [128, 128], "float32"),
+    "crow": ("sbuf", [128, 256], "float32"),
+    "jrow": ("sbuf", [128, 256], "float32"),
+    "lq": ("sbuf", [128, NB * 128], "float32"),
+    "rc": ("sbuf", [128, NB * 256], "float32"),
+    "inv": ("sbuf", [128, 256], "uint16"),
+    "ps_s": ("psum", [128, 512], "float32"),
+    "ps_i": ("psum", [128, 512], "float32"),
+}
+SEMAPHORES = (["gi", "v", "lsnd", "lplc", "lx", "lg", "sndr", "t1", "ofsr", "t2", "invr", "g0", "g1",
+               "rel", "sent", "arr", "st"]
+              + ["oh%d" % b for b in range(NB)] + ["yr%d" % k for k in range(len(BLOCKS))])
+
+
+def bits(m):
+    return [e for e in range(m.bit_length()) if (m >> e) & 1]
+
+
+def mask_of(engines):
+    m = 0
+    for e in engines:
+        m |= 1 << e
+    return m
+
+
+def routes(T, topo, r):
+    n = len(T.cores)
+    me = T.cores[r]
+    nbr = [T.cores[(r - 1) % n], T.cores[(r + 1) % n]]
+    own = [c for c in range(SIM) if c != me and topo.chip(c) == topo.chip(me) and all(topo.may_write(c, d) for d in nbr)]
+    near = [c for c in own if topo.die(c) == topo.die(me)]
+    far = [c for c in own if topo.die(c) != topo.die(me)]
+    order = sorted((0, 1), key=lambda s: (topo.may_write(me, nbr[s]), topo.mates(topo.chip(me), topo.chip(nbr[s]))))
+    calls = []
+    for s in order:
+        d = nbr[s]
+        calls.append([dict(side=s, part=1, dst=d, via=far[s]),
+                      dict(side=s, part=0, dst=d, via=None if topo.may_write(me, d) else near[s])])
+    both = bits(topo.mask(me, far[0]))
+    m = topo.mask(me, far[0])
+    for t in calls[1]:
+        m &= topo.mask(me, t["dst"] if t["via"] is None else t["via"])
+    late = bits(m)[:len(both) // 2]
+    early = [e for e in both if e not in late]
+    for pool, call in ((early, calls[0]), (late, calls[1])):
+        call[0]["eng"] = pool[0::2]
+        call[1]["eng"] = pool[1::2]
+    return calls
+
+
+def landing(t):
+    a = W + (CAP if t["side"] == 0 else 0) + t["part"] * HALF
+    return a, a + HALF
+
+
+def relay_program(g, core, T, topo):
+    for r in range(len(T.cores)):
+        for call in routes(T, topo, r):
+            for t in call:
+                if t["via"] != core:
+                    continue
+                m = topo.mask(core, t["dst"])
+                rid, pid, _ = topo.addr(t["dst"])
+                a, b = landing(t)
+                g.wait_ge(T.sem.rel, len(t["eng"]))
+                g.remote_dma(T.tab[:, a:b], T.relay[:], T.sem.arr, T.sem.sent, pid, rid, m)
+                g.wait_ge(T.sem.sent, len(bits(m)))
+
+
+def rank_program(g, core, T, topo):
+    rank = T.rank_of(core)
+    if rank is None:
+        relay_program(g, core, T, topo)
+        return
+    sem = T.sem
+    calls = routes(T, topo, rank)
+    arrivals = 0
+    for r in range(len(T.cores)):
+        for call in routes(T, topo, r):
+            for t in call:
+                if t["dst"] == core:
+                    arrivals += len(t["eng"]) if t["via"] is None else len(bits(topo.mask(t["via"], core)))
+
+    g.sync.dma_start(T.sndi[0:16, :], T.snd[:]).then_inc(sem.lsnd, 16)
+    g.scalar.dma_start(T.plci[:], T.plc[:]).then_inc(sem.lplc, 16)
+    g.sync.dma_start(T.xs[:], T.x[:]).then_inc(sem.lx, 16)
+    g.sync.dma_start(T.tab[0:64, 0:W], T.gh[0:64, :]).then_inc(sem.lg, 16)
+    nsent = sum(len(t["eng"]) for call in calls for t in call)
+    g.sync.wait_ge(sem.sent, nsent)
+    g.sync.dma_start(T.tab[64:128, 0:W], T.gh[64:128, :]).then_inc(sem.lg, 16)
+
+    g.iota(T.pidx[:], [[1, 1]], 0, 1).then_inc(sem.gi, 1)
+    g.iota(T.qrow[:], [[0, 8], [1, 16]], 0, 0, allow_small_or_imprecise_dtypes=True).then_inc(sem.gi, 1)
+    g.iota(T.ib[:], [[16, NB]], W, 0, allow_small_or_imprecise_dtypes=True).then_inc(sem.gi, 1)
+    g.iota(T.crow[:], [[1, 256]], 0, 0, allow_small_or_imprecise_dtypes=True).then_inc(sem.gi, 1)
+    g.iota(T.jrow[0:16, :], [[16, 256]], 0, 1, allow_small_or_imprecise_dtypes=True).then_inc(sem.gi, 1)
+
+    v = g.vector
+    n = [0]
+
+    def step(call):
+        call.then_inc(sem.v, 1)
+        n[0] += 1
+
+    def settle():
+        v.wait_ge(sem.v, n[0])
+
+    v.wait_ge(sem.gi, 5)
+    step(v.tensor_scalar(T.mi[:], T.pidx[:], 7, None, AluOpType.bitwise_and))
+    step(v.tensor_scalar(T.qi[:], T.pidx[:], 3, None, AluOpType.logical_shift_right))
+    step(v.tensor_copy(T.pf[:], T.pidx[:]))
+    settle()
+    step(v.tensor_scalar(T.mf[:], T.mi[:], 128, None, AluOpType.mult))
+    step(v.tensor_copy(T.qf[:], T.qi[:]))
+    step(v.tensor_scalar(T.rr[0:16, :], T.qrow[0:16, :], T.pf[0:16, :], None, AluOpType.is_equal))
+    settle()
+    step(v.tensor_scalar(T.iv[:], T.ib[:], T.mf[:], T.qf[:], AluOpType.add, AluOpType.add))
+    settle()
+
+    v.wait_ge(sem.lsnd, 16)
+    v.tensor_copy(T.sndf[0:16, :], T.sndi[0:16, :]).then_inc(sem.sndr, 1)
+    g.tensor.wait_ge(sem.sndr, 1)
+    g.tensor.matmul(T.ps_s[:, 0:64], T.rr[0:16, :], T.sndf[0:16, :], True, True).then_inc(sem.t1, 1)
+    v.wait_ge(sem.lplc, 16)
+    step(v.tensor_scalar(T.phi[:], T.plci[:], 4, None, AluOpType.logical_shift_right))
+    step(v.tensor_scalar(T.pli[:], T.plci[:], 15, None, AluOpType.bitwise_and))
+    step(v.tensor_copy(T.plcf[:], T.plci[:]))
+    settle()
+    v.wait_ge(sem.t1, 1)
+    v.tensor_copy(T.ofs[:], T.ps_s[:, 0:64]).then_inc(sem.ofsr, 1)
+    step(v.tensor_copy(T.phf[:], T.phi[:]))
+    step(v.tensor_copy(T.plf[:], T.pli[:]))
+    step(v.tensor_tensor(T.val[:], T.iv[:], T.plcf[:], AluOpType.subtract))
+    settle()
+
+    for b in range(NB):
+        s = sem["oh%d" % b]
+        v.tensor_scalar(T.lq[:, 128 * b:128 * (b + 1)], T.qrow[:], T.plf[:, b:b + 1], None, AluOpType.is_equal).then_inc(s, 1)
+        v.tensor_scalar(T.rc[:, 256 * b:256 * (b + 1)], T.crow[:], T.phf[:, b:b + 1], T.val[:, b:b + 1],
+                        AluOpType.is_equal, AluOpType.mult).then_inc(s, 1)
+    g.tensor.matmul(T.ps_i[:, 0:256], T.rr[0:16, :], T.jrow[0:16, :], True, False)
+    for b in range(NB):
+        g.tensor.wait_ge(sem["oh%d" % b], 2)
+        mm = g.tensor.matmul(T.ps_i[:, 0:256], T.lq[:, 128 * b:128 * (b + 1)], T.rc[:, 256 * b:256 * (b + 1)],
+                             False, b == NB - 1)
+    mm.then_inc(sem.t2, 1)
+
+    v.wait_ge(sem.lx, 16)
+    v.wait_ge(sem.ofsr, 1)
+    g.scalar.wait_ge(sem.lx, 16)
+    g.scalar.wait_ge(sem.ofsr, 1)
+    for k, call in enumerate(calls):
+        side = call[0]["side"]
+        c, e = CAP * side, 32 * side
+        v.tensor_copy(T.outb[:, c:c + HALF], T.xs[:].indirect(T.ofs[:, e:e + 16])).then_inc(sem["g%d" % k], 1)
+        g.scalar.activation(T.outb[:, c + HALF:c + CAP], T.xs[:].indirect(T.ofs[:, e + 16:e + 32]),
+                            ActivationFunctionType.Copy).then_inc(sem["g%d" % k], 1)
+        g.wait_ge(sem["g%d" % k], 2)
+        transfers = []
+        for t in call:
+            src = T.outb[:, c + t["part"] * HALF:c + (t["part"] + 1) * HALF]
+            if t["via"] is None:
+                a, b = landing(t)
+                to, dst, rs = t["dst"], T.tab[:, a:b], sem.arr
+            else:
+                to, dst, rs = t["via"], T.relay[:], sem.rel
+            rid, pid, _ = topo.addr(to)
+            transfers.append(RemoteDMATransfer(dst_ids=[DstId(rid=rid, pnc=pid)], dma_engine_mask=mask_of(t["eng"]),
+                                               remote_sem=rs, src=src, dst=dst))
+        g.remote_dma_fused(transfers, local_sem=sem.sent)
+    g.wait_ge(sem.sent, nsent)
+
+    v.wait_ge(sem.t2, 1)
+    v.tensor_copy(T.inv[:], T.ps_i[:, 0:256]).then_inc(sem.invr, 1)
+    for q in (v, g.scalar):
+        q.wait_ge(sem.invr, 1)
+        q.wait_ge(sem.lg, 32)
+        q.wait_ge(sem.arr, arrivals)
+    j = 0
+    for k, width in enumerate(BLOCKS):
+        h = width // 2
+        s = sem["yr%d" % k]
+        v.tensor_copy(T.ys[:, j:j + h], T.tab[:].indirect(T.inv[:, j // 16:(j + h) // 16])).then_inc(s, 1)
+        g.scalar.activation(T.ys[:, j + h:j + width], T.tab[:].indirect(T.inv[:, (j + h) // 16:(j + width) // 16]),
+                            ActivationFunctionType.Copy).then_inc(s, 1)
+        g.sync.wait_ge(s, 2)
+        g.sync.dma_start(T.y[:, j:j + width], T.ys[:, j:j + width]).then_inc(sem.st, 16)
+        j += width
+    g.sync.wait_ge(sem.st, 16 * len(BLOCKS))

@@ -4,7 +4,11 @@ from concourse.mybir import AluOpType, ActivationFunctionType
 SIM = 96
 W, CAP, HALF = 4096, 512, 256
 NB = 8
-BLOCKS = (640, 1216, 2240)
+NH = 4
+QC = 256 // NH
+BLOCKS = (640, 896, 1280, 1280)
+STARTS = [W - sum(BLOCKS[:_k + 1]) for _k in range(len(BLOCKS))]
+EARLY = 2
 
 SCRATCH = {
     "xs": ("sbuf", [128, W], "float32"),
@@ -15,33 +19,27 @@ SCRATCH = {
     "sndi": ("sbuf", [128, 64], "int32"),
     "sndf": ("sbuf", [128, 64], "float32"),
     "ofs": ("sbuf", [128, 64], "uint16"),
-    "plci": ("sbuf", [128, NB], "int32"),
-    "plcf": ("sbuf", [128, NB], "float32"),
-    "phi": ("sbuf", [128, NB], "int32"),
-    "pli": ("sbuf", [128, NB], "int32"),
-    "phf": ("sbuf", [128, NB], "float32"),
-    "plf": ("sbuf", [128, NB], "float32"),
-    "val": ("sbuf", [128, NB], "float32"),
-    "ib": ("sbuf", [128, NB], "float32"),
-    "iv": ("sbuf", [128, NB], "float32"),
-    "pidx": ("sbuf", [128, 1], "int32"),
-    "mi": ("sbuf", [128, 1], "int32"),
-    "qi": ("sbuf", [128, 1], "int32"),
-    "pf": ("sbuf", [128, 1], "float32"),
-    "mf": ("sbuf", [128, 1], "float32"),
-    "qf": ("sbuf", [128, 1], "float32"),
     "qrow": ("sbuf", [128, 128], "float32"),
     "rr": ("sbuf", [128, 128], "float32"),
-    "crow": ("sbuf", [128, 256], "float32"),
-    "jrow": ("sbuf", [128, 256], "float32"),
+    "crow": ("sbuf", [128, QC], "float32"),
+    "jrow": ("sbuf", [128, QC], "float32"),
     "lq": ("sbuf", [128, NB * 128], "float32"),
-    "rc": ("sbuf", [128, NB * 256], "float32"),
-    "inv": ("sbuf", [128, 256], "uint16"),
+    "rc": ("sbuf", [128, NB * QC], "float32"),
+    "part": ("sbuf", [128, QC], "uint16"),
+    "inv": ("sbuf", [128, NH * QC], "uint16"),
     "ps_s": ("psum", [128, 512], "float32"),
     "ps_i": ("psum", [128, 512], "float32"),
 }
-SEMAPHORES = (["gi", "v", "lsnd", "lplc", "lx", "lg", "sndr", "t1", "ofsr", "t2", "invr", "g0", "g1",
-               "rel", "sent", "arr", "st"]
+for _name in ("plci", "phi", "pli"):
+    SCRATCH[_name] = ("sbuf", [128, NB], "int32")
+for _name in ("plcf", "phf", "plf", "val", "ib", "iv"):
+    SCRATCH[_name] = ("sbuf", [128, NB], "float32")
+for _name in ("pidx", "mi", "qi"):
+    SCRATCH[_name] = ("sbuf", [128, 1], "int32")
+for _name in ("pf", "mf", "qf"):
+    SCRATCH[_name] = ("sbuf", [128, 1], "float32")
+SEMAPHORES = (["gi", "v", "lsnd", "lplc", "lx", "lga", "lgb", "sndr", "t1", "ofsr", "t2", "pl", "psent", "partr",
+               "isent", "invr", "g0", "g1", "rel", "sent", "arr", "st"]
               + ["oh%d" % b for b in range(NB)] + ["yr%d" % k for k in range(len(BLOCKS))])
 
 
@@ -56,28 +54,30 @@ def mask_of(engines):
     return m
 
 
-def routes(T, topo, r):
+def neighbours(T, r):
     n = len(T.cores)
+    return [T.cores[(r - 1) % n], T.cores[(r + 1) % n]]
+
+
+def helpers(T, topo, r):
     me = T.cores[r]
-    nbr = [T.cores[(r - 1) % n], T.cores[(r + 1) % n]]
-    own = [c for c in range(SIM) if c != me and topo.chip(c) == topo.chip(me) and all(topo.may_write(c, d) for d in nbr)]
-    near = [c for c in own if topo.die(c) == topo.die(me)]
-    far = [c for c in own if topo.die(c) != topo.die(me)]
+    own = [c for c in range(SIM) if c != me and topo.chip(c) == topo.chip(me)
+           and all(topo.may_write(c, d) for d in neighbours(T, r))]
+    return ([c for c in own if topo.die(c) == topo.die(me)], [c for c in own if topo.die(c) != topo.die(me)])
+
+
+def routes(T, topo, r):
+    me = T.cores[r]
+    nbr = neighbours(T, r)
+    near, far = helpers(T, topo, r)
     order = sorted((0, 1), key=lambda s: (topo.may_write(me, nbr[s]), topo.mates(topo.chip(me), topo.chip(nbr[s]))))
     calls = []
     for s in order:
         d = nbr[s]
-        calls.append([dict(side=s, part=1, dst=d, via=far[s]),
-                      dict(side=s, part=0, dst=d, via=None if topo.may_write(me, d) else near[s])])
-    both = bits(topo.mask(me, far[0]))
-    m = topo.mask(me, far[0])
-    for t in calls[1]:
-        m &= topo.mask(me, t["dst"] if t["via"] is None else t["via"])
-    late = bits(m)[:len(both) // 2]
-    early = [e for e in both if e not in late]
-    for pool, call in ((early, calls[0]), (late, calls[1])):
-        call[0]["eng"] = pool[0::2]
-        call[1]["eng"] = pool[1::2]
+        via = None if topo.may_write(me, d) else near[s]
+        ef = bits(topo.mask(me, far[s]))[0::2]
+        en = [e for e in bits(topo.mask(me, d if via is None else via)) if e not in ef]
+        calls.append([dict(side=s, part=1, dst=d, via=far[s], eng=ef), dict(side=s, part=0, dst=d, via=via, eng=en)])
     return calls
 
 
@@ -86,8 +86,28 @@ def landing(t):
     return a, a + HALF
 
 
-def relay_program(g, core, T, topo):
+class Steps:
+    pass
+
+
+def counter(q, sem):
+    n = [0]
+
+    def step(call):
+        call.then_inc(sem, 1)
+        n[0] += 1
+
+    def settle():
+        q.wait_ge(sem, n[0])
+
+    return step, settle
+
+
+def helper_program(g, core, T, topo):
     for r in range(len(T.cores)):
+        near, far = helpers(T, topo, r)
+        if core in near + far:
+            invert(g, core, T, topo, T.cores[r], (near + far).index(core), neighbours(T, r))
         for call in routes(T, topo, r):
             for t in call:
                 if t["via"] != core:
@@ -98,46 +118,27 @@ def relay_program(g, core, T, topo):
                 g.wait_ge(T.sem.rel, len(t["eng"]))
                 g.remote_dma(T.tab[:, a:b], T.relay[:], T.sem.arr, T.sem.sent, pid, rid, m)
                 g.wait_ge(T.sem.sent, len(bits(m)))
+        if core in near + far:
+            g.wait_ge(T.sem.isent, len(back_engines(topo, core, neighbours(T, r))))
 
 
-def rank_program(g, core, T, topo):
-    rank = T.rank_of(core)
-    if rank is None:
-        relay_program(g, core, T, topo)
-        return
-    sem = T.sem
-    calls = routes(T, topo, rank)
-    arrivals = 0
-    for r in range(len(T.cores)):
-        for call in routes(T, topo, r):
-            for t in call:
-                if t["dst"] == core:
-                    arrivals += len(t["eng"]) if t["via"] is None else len(bits(topo.mask(t["via"], core)))
+def back_engines(topo, core, nbr):
+    return bits(topo.mask(core, nbr[0]) & topo.mask(core, nbr[1]))
 
-    g.sync.dma_start(T.sndi[0:16, :], T.snd[:]).then_inc(sem.lsnd, 16)
-    g.scalar.dma_start(T.plci[:], T.plc[:]).then_inc(sem.lplc, 16)
-    g.sync.dma_start(T.xs[:], T.x[:]).then_inc(sem.lx, 16)
-    g.sync.dma_start(T.tab[0:64, 0:W], T.gh[0:64, :]).then_inc(sem.lg, 16)
-    nsent = sum(len(t["eng"]) for call in calls for t in call)
-    g.sync.wait_ge(sem.sent, nsent)
-    g.sync.dma_start(T.tab[64:128, 0:W], T.gh[64:128, :]).then_inc(sem.lg, 16)
 
+def plc_engines(topo, me, cores, k):
+    return bits(topo.mask(me, cores[k]))[k::len(cores)]
+
+
+def invert(g, core, T, topo, owner, k, nbr):
+    sem, v = T.sem, g.vector
+    step, settle = counter(v, sem.v)
+    flag = dict(allow_small_or_imprecise_dtypes=True)
     g.iota(T.pidx[:], [[1, 1]], 0, 1).then_inc(sem.gi, 1)
-    g.iota(T.qrow[:], [[0, 8], [1, 16]], 0, 0, allow_small_or_imprecise_dtypes=True).then_inc(sem.gi, 1)
-    g.iota(T.ib[:], [[16, NB]], W, 0, allow_small_or_imprecise_dtypes=True).then_inc(sem.gi, 1)
-    g.iota(T.crow[:], [[1, 256]], 0, 0, allow_small_or_imprecise_dtypes=True).then_inc(sem.gi, 1)
-    g.iota(T.jrow[0:16, :], [[16, 256]], 0, 1, allow_small_or_imprecise_dtypes=True).then_inc(sem.gi, 1)
-
-    v = g.vector
-    n = [0]
-
-    def step(call):
-        call.then_inc(sem.v, 1)
-        n[0] += 1
-
-    def settle():
-        v.wait_ge(sem.v, n[0])
-
+    g.iota(T.qrow[:], [[0, 8], [1, 16]], 0, 0, **flag).then_inc(sem.gi, 1)
+    g.iota(T.ib[:], [[16, NB]], W, 0, **flag).then_inc(sem.gi, 1)
+    g.iota(T.crow[:], [[1, QC]], QC * k, 0, **flag).then_inc(sem.gi, 1)
+    g.iota(T.jrow[0:16, :], [[16, QC]], 16 * QC * k, 1, **flag).then_inc(sem.gi, 1)
     v.wait_ge(sem.gi, 5)
     step(v.tensor_scalar(T.mi[:], T.pidx[:], 7, None, AluOpType.bitwise_and))
     step(v.tensor_scalar(T.qi[:], T.pidx[:], 3, None, AluOpType.logical_shift_right))
@@ -149,39 +150,93 @@ def rank_program(g, core, T, topo):
     settle()
     step(v.tensor_scalar(T.iv[:], T.ib[:], T.mf[:], T.qf[:], AluOpType.add, AluOpType.add))
     settle()
-
-    v.wait_ge(sem.lsnd, 16)
-    v.tensor_copy(T.sndf[0:16, :], T.sndi[0:16, :]).then_inc(sem.sndr, 1)
-    g.tensor.wait_ge(sem.sndr, 1)
-    g.tensor.matmul(T.ps_s[:, 0:64], T.rr[0:16, :], T.sndf[0:16, :], True, True).then_inc(sem.t1, 1)
-    v.wait_ge(sem.lplc, 16)
+    v.wait_ge(sem.pl, len(plc_engines(topo, owner, [core] * NH, k)))
     step(v.tensor_scalar(T.phi[:], T.plci[:], 4, None, AluOpType.logical_shift_right))
     step(v.tensor_scalar(T.pli[:], T.plci[:], 15, None, AluOpType.bitwise_and))
     step(v.tensor_copy(T.plcf[:], T.plci[:]))
     settle()
-    v.wait_ge(sem.t1, 1)
-    v.tensor_copy(T.ofs[:], T.ps_s[:, 0:64]).then_inc(sem.ofsr, 1)
     step(v.tensor_copy(T.phf[:], T.phi[:]))
     step(v.tensor_copy(T.plf[:], T.pli[:]))
     step(v.tensor_tensor(T.val[:], T.iv[:], T.plcf[:], AluOpType.subtract))
     settle()
-
     for b in range(NB):
         s = sem["oh%d" % b]
-        v.tensor_scalar(T.lq[:, 128 * b:128 * (b + 1)], T.qrow[:], T.plf[:, b:b + 1], None, AluOpType.is_equal).then_inc(s, 1)
-        v.tensor_scalar(T.rc[:, 256 * b:256 * (b + 1)], T.crow[:], T.phf[:, b:b + 1], T.val[:, b:b + 1],
+        v.tensor_scalar(T.lq[:, 128 * b:128 * (b + 1)], T.qrow[:], T.plf[:, b:b + 1], None,
+                        AluOpType.is_equal).then_inc(s, 1)
+        v.tensor_scalar(T.rc[:, QC * b:QC * (b + 1)], T.crow[:], T.phf[:, b:b + 1], T.val[:, b:b + 1],
                         AluOpType.is_equal, AluOpType.mult).then_inc(s, 1)
-    g.tensor.matmul(T.ps_i[:, 0:256], T.rr[0:16, :], T.jrow[0:16, :], True, False)
     for b in range(NB):
         g.tensor.wait_ge(sem["oh%d" % b], 2)
-        mm = g.tensor.matmul(T.ps_i[:, 0:256], T.lq[:, 128 * b:128 * (b + 1)], T.rc[:, 256 * b:256 * (b + 1)],
+        if b == 0:
+            g.tensor.matmul(T.ps_i[:, 0:QC], T.rr[0:16, :], T.jrow[0:16, :], True, False)
+        mm = g.tensor.matmul(T.ps_i[:, 0:QC], T.lq[:, 128 * b:128 * (b + 1)], T.rc[:, QC * b:QC * (b + 1)],
                              False, b == NB - 1)
     mm.then_inc(sem.t2, 1)
+    v.wait_ge(sem.t2, 1)
+    pieces = 0
+    for j, width in zip(STARTS, BLOCKS):
+        a, e = max(j // 16, QC * k) - QC * k, min((j + width) // 16, QC * (k + 1)) - QC * k
+        if a < e:
+            v.tensor_scalar(T.part[:, a:e], T.ps_i[:, a:e], j, None, AluOpType.subtract).then_inc(sem.partr, 1)
+            pieces += 1
+    g.wait_ge(sem.partr, pieces)
+    rid, pid, _ = topo.addr(owner)
+    g.remote_dma(T.inv[:, QC * k:QC * (k + 1)], T.part[:], sem.invr, sem.isent, pid, rid,
+                 mask_of(back_engines(topo, core, nbr)))
 
-    v.wait_ge(sem.lx, 16)
-    v.wait_ge(sem.ofsr, 1)
-    g.scalar.wait_ge(sem.lx, 16)
-    g.scalar.wait_ge(sem.ofsr, 1)
+
+def rank_program(g, core, T, topo):
+    rank = T.rank_of(core)
+    if rank is None:
+        helper_program(g, core, T, topo)
+        return
+    sem, v = T.sem, g.vector
+    calls = routes(T, topo, rank)
+    near, far = helpers(T, topo, rank)
+    help4 = near + far
+    arrivals = 0
+    for r in range(len(T.cores)):
+        for call in routes(T, topo, r):
+            for t in call:
+                if t["dst"] == core:
+                    arrivals += len(t["eng"]) if t["via"] is None else len(bits(topo.mask(t["via"], core)))
+    nsent = sum(len(t["eng"]) for call in calls for t in call)
+    ninv = sum(len(back_engines(topo, h, neighbours(T, rank))) for h in help4)
+
+    cut = STARTS[EARLY - 1]
+    g.sync.dma_start(T.sndi[0:16, :], T.snd[:]).then_inc(sem.lsnd, 16)
+    g.scalar.dma_start(T.plci[:], T.plc[:]).then_inc(sem.lplc, 16)
+    g.sync.dma_start(T.xs[:], T.x[:]).then_inc(sem.lx, 16)
+    g.sync.dma_start(T.tab[:, cut:W], T.gh[:, cut:W]).then_inc(sem.lga, 16)
+    g.sync.wait_ge(sem.sent, nsent)
+    g.sync.dma_start(T.tab[:, 0:cut], T.gh[:, 0:cut]).then_inc(sem.lgb, 16)
+
+    g.iota(T.pidx[:], [[1, 1]], 0, 1).then_inc(sem.gi, 1)
+    g.iota(T.qrow[:], [[0, 8], [1, 16]], 0, 0, allow_small_or_imprecise_dtypes=True).then_inc(sem.gi, 1)
+    g.wait_ge(sem.lplc, 16)
+    transfers = []
+    for k, h in enumerate(help4):
+        rid, pid, _ = topo.addr(h)
+        transfers.append(RemoteDMATransfer(dst_ids=[DstId(rid=rid, pnc=pid)], remote_sem=sem.pl, src=T.plci[:], dst=T.plci[:],
+                                           dma_engine_mask=mask_of(plc_engines(topo, core, help4, k))))
+    g.remote_dma_fused(transfers, local_sem=sem.psent)
+
+    step, settle = counter(v, sem.v)
+    v.wait_ge(sem.gi, 2)
+    step(v.tensor_copy(T.pf[:], T.pidx[:]))
+    settle()
+    step(v.tensor_scalar(T.rr[0:16, :], T.qrow[0:16, :], T.pf[0:16, :], None, AluOpType.is_equal))
+    settle()
+    v.wait_ge(sem.lsnd, 16)
+    v.tensor_copy(T.sndf[0:16, :], T.sndi[0:16, :]).then_inc(sem.sndr, 1)
+    g.tensor.wait_ge(sem.sndr, 1)
+    g.tensor.matmul(T.ps_s[:, 0:64], T.rr[0:16, :], T.sndf[0:16, :], True, True).then_inc(sem.t1, 1)
+    v.wait_ge(sem.t1, 1)
+    v.tensor_copy(T.ofs[:], T.ps_s[:, 0:64]).then_inc(sem.ofsr, 1)
+
+    for q in (v, g.scalar):
+        q.wait_ge(sem.lx, 16)
+        q.wait_ge(sem.ofsr, 1)
     for k, call in enumerate(calls):
         side = call[0]["side"]
         c, e = CAP * side, 32 * side
@@ -202,21 +257,22 @@ def rank_program(g, core, T, topo):
                                                remote_sem=rs, src=src, dst=dst))
         g.remote_dma_fused(transfers, local_sem=sem.sent)
     g.wait_ge(sem.sent, nsent)
+    g.wait_ge(sem.psent, sum(len(plc_engines(topo, core, help4, k)) for k in range(NH)))
 
-    v.wait_ge(sem.t2, 1)
-    v.tensor_copy(T.inv[:], T.ps_i[:, 0:256]).then_inc(sem.invr, 1)
     for q in (v, g.scalar):
-        q.wait_ge(sem.invr, 1)
-        q.wait_ge(sem.lg, 32)
+        q.wait_ge(sem.invr, ninv)
+        q.wait_ge(sem.lga, 16)
         q.wait_ge(sem.arr, arrivals)
-    j = 0
-    for k, width in enumerate(BLOCKS):
-        h = width // 2
+    for k, (j, width) in enumerate(zip(STARTS, BLOCKS)):
+        h = j + width // 2
         s = sem["yr%d" % k]
-        v.tensor_copy(T.ys[:, j:j + h], T.tab[:].indirect(T.inv[:, j // 16:(j + h) // 16])).then_inc(s, 1)
-        g.scalar.activation(T.ys[:, j + h:j + width], T.tab[:].indirect(T.inv[:, (j + h) // 16:(j + width) // 16]),
+        win = T.tab[:, j:W + 2 * CAP]
+        if k == EARLY:
+            v.wait_ge(sem.lgb, 16)
+            g.scalar.wait_ge(sem.lgb, 16)
+        v.tensor_copy(T.ys[:, j:h], win.indirect(T.inv[:, j // 16:h // 16])).then_inc(s, 1)
+        g.scalar.activation(T.ys[:, h:j + width], win.indirect(T.inv[:, h // 16:(j + width) // 16]),
                             ActivationFunctionType.Copy).then_inc(s, 1)
         g.sync.wait_ge(s, 2)
         g.sync.dma_start(T.y[:, j:j + width], T.ys[:, j:j + width]).then_inc(sem.st, 16)
-        j += width
     g.sync.wait_ge(sem.st, 16 * len(BLOCKS))

@@ -38,8 +38,8 @@ for _name in ("pidx", "mi", "qi"):
     SCRATCH[_name] = ("sbuf", [128, 1], "int32")
 for _name in ("pf", "mf", "qf"):
     SCRATCH[_name] = ("sbuf", [128, 1], "float32")
-SEMAPHORES = (["gi", "v", "lsnd", "lplc", "lx", "lga", "lgb", "sndr", "t1", "ofsr", "t2", "pl", "psent", "partr",
-               "isent", "invr", "g0", "g1", "rel", "sent", "arr", "st"]
+SEMAPHORES = (["gi", "v", "lsnd", "lplc", "lx", "lga", "lgb", "sndr", "t1", "ofsr", "t2", "pl", "pgo", "psent", "partr",
+               "isent", "invr", "g0", "g1", "rel", "sent0", "sent1", "arr", "st"]
               + ["oh%d" % b for b in range(NB)] + ["yr%d" % k for k in range(len(BLOCKS))])
 
 
@@ -86,10 +86,6 @@ def landing(t):
     return a, a + HALF
 
 
-class Steps:
-    pass
-
-
 def counter(q, sem):
     n = [0]
 
@@ -116,8 +112,8 @@ def helper_program(g, core, T, topo):
                 rid, pid, _ = topo.addr(t["dst"])
                 a, b = landing(t)
                 g.wait_ge(T.sem.rel, len(t["eng"]))
-                g.remote_dma(T.tab[:, a:b], T.relay[:], T.sem.arr, T.sem.sent, pid, rid, m)
-                g.wait_ge(T.sem.sent, len(bits(m)))
+                g.remote_dma(T.tab[:, a:b], T.relay[:], T.sem.arr, T.sem.sent0, pid, rid, m)
+                g.wait_ge(T.sem.sent0, len(bits(m)))
         if core in near + far:
             g.wait_ge(T.sem.isent, len(back_engines(topo, core, neighbours(T, r))))
 
@@ -200,15 +196,17 @@ def rank_program(g, core, T, topo):
             for t in call:
                 if t["dst"] == core:
                     arrivals += len(t["eng"]) if t["via"] is None else len(bits(topo.mask(t["via"], core)))
-    nsent = sum(len(t["eng"]) for call in calls for t in call)
+    nsent = [sum(len(t["eng"]) for t in call) for call in calls]
     ninv = sum(len(back_engines(topo, h, neighbours(T, rank))) for h in help4)
 
     cut = STARTS[EARLY - 1]
     g.sync.dma_start(T.sndi[0:16, :], T.snd[:]).then_inc(sem.lsnd, 16)
     g.scalar.dma_start(T.plci[:], T.plc[:]).then_inc(sem.lplc, 16)
     g.sync.dma_start(T.xs[:], T.x[:]).then_inc(sem.lx, 16)
+    g.sync.wait_ge(sem.pgo, 1)
+    g.sync.wait_ge(sem.ofsr, 1)
     g.sync.dma_start(T.tab[:, cut:W], T.gh[:, cut:W]).then_inc(sem.lga, 16)
-    g.sync.wait_ge(sem.sent, nsent)
+    g.sync.wait_ge(sem.sent0, nsent[0])
     g.sync.dma_start(T.tab[:, 0:cut], T.gh[:, 0:cut]).then_inc(sem.lgb, 16)
 
     g.iota(T.pidx[:], [[1, 1]], 0, 1).then_inc(sem.gi, 1)
@@ -220,6 +218,7 @@ def rank_program(g, core, T, topo):
         transfers.append(RemoteDMATransfer(dst_ids=[DstId(rid=rid, pnc=pid)], remote_sem=sem.pl, src=T.plci[:], dst=T.plci[:],
                                            dma_engine_mask=mask_of(plc_engines(topo, core, help4, k))))
     g.remote_dma_fused(transfers, local_sem=sem.psent)
+    g.sem_inc(sem.pgo, 1)
 
     step, settle = counter(v, sem.v)
     v.wait_ge(sem.gi, 2)
@@ -255,8 +254,9 @@ def rank_program(g, core, T, topo):
             rid, pid, _ = topo.addr(to)
             transfers.append(RemoteDMATransfer(dst_ids=[DstId(rid=rid, pnc=pid)], dma_engine_mask=mask_of(t["eng"]),
                                                remote_sem=rs, src=src, dst=dst))
-        g.remote_dma_fused(transfers, local_sem=sem.sent)
-    g.wait_ge(sem.sent, nsent)
+        g.remote_dma_fused(transfers, local_sem=sem["sent%d" % k])
+    for k in range(len(calls)):
+        g.wait_ge(sem["sent%d" % k], nsent[k])
     g.wait_ge(sem.psent, sum(len(plc_engines(topo, core, help4, k)) for k in range(NH)))
 
     for q in (v, g.scalar):

@@ -4,9 +4,10 @@ from concourse.mybir import AluOpType, ActivationFunctionType
 SIM = 96
 W, CAP, HALF = 4096, 512, 256
 NB = 8
-NH = 4
+VB = 5
+NH = 2
 QC = 256 // NH
-BLOCKS = (640, 896, 1280, 1280)
+BLOCKS = (640, 1024, 1280, 1152)
 STARTS = [W - sum(BLOCKS[:_k + 1]) for _k in range(len(BLOCKS))]
 EARLY = 2
 
@@ -24,23 +25,26 @@ SCRATCH = {
     "crow": ("sbuf", [128, QC], "float32"),
     "jrow": ("sbuf", [128, QC], "float32"),
     "lq": ("sbuf", [128, NB * 128], "float32"),
+    "ab": ("sbuf", [128, (NB - VB) * 128], "float32"),
     "rc": ("sbuf", [128, NB * QC], "float32"),
     "part": ("sbuf", [128, QC], "uint16"),
     "inv": ("sbuf", [128, NH * QC], "uint16"),
+    "pv": ("sbuf", [128, 3 * NB], "float32"),
     "ps_s": ("psum", [128, 512], "float32"),
     "ps_i": ("psum", [128, 512], "float32"),
 }
 for _name in ("plci", "phi", "pli"):
     SCRATCH[_name] = ("sbuf", [128, NB], "int32")
-for _name in ("plcf", "phf", "plf", "val", "ib", "iv"):
+for _name in ("plcf", "ib", "iv"):
     SCRATCH[_name] = ("sbuf", [128, NB], "float32")
 for _name in ("pidx", "mi", "qi"):
     SCRATCH[_name] = ("sbuf", [128, 1], "int32")
 for _name in ("pf", "mf", "qf"):
     SCRATCH[_name] = ("sbuf", [128, 1], "float32")
-SEMAPHORES = (["gi", "v", "lsnd", "lplc", "lx", "lga", "lgb", "sndr", "t1", "ofsr", "t2", "pl", "pgo", "psent", "partr",
-               "isent", "invr", "g0", "g1", "rel", "sent0", "sent1", "arr", "st"]
+SEMAPHORES = (["gi", "v", "lsnd", "lplc", "lx", "lga", "lgb", "sndr", "t1", "ofsr", "t2", "pl", "pvr", "abr", "ggo",
+               "psent", "partr", "isent", "invr", "g0", "g1", "rel", "sent", "arr", "st"]
               + ["oh%d" % b for b in range(NB)] + ["yr%d" % k for k in range(len(BLOCKS))])
+FLAG = dict(allow_small_or_imprecise_dtypes=True)
 
 
 def bits(m):
@@ -59,17 +63,12 @@ def neighbours(T, r):
     return [T.cores[(r - 1) % n], T.cores[(r + 1) % n]]
 
 
-def helpers(T, topo, r):
-    me = T.cores[r]
-    own = [c for c in range(SIM) if c != me and topo.chip(c) == topo.chip(me)
-           and all(topo.may_write(c, d) for d in neighbours(T, r))]
-    return ([c for c in own if topo.die(c) == topo.die(me)], [c for c in own if topo.die(c) != topo.die(me)])
-
-
-def routes(T, topo, r):
+def plan(T, topo, r):
     me = T.cores[r]
     nbr = neighbours(T, r)
-    near, far = helpers(T, topo, r)
+    own = [c for c in range(SIM) if c != me and topo.chip(c) == topo.chip(me) and all(topo.may_write(c, d) for d in nbr)]
+    near = [c for c in own if topo.die(c) == topo.die(me)]
+    far = [c for c in own if topo.die(c) != topo.die(me)]
     order = sorted((0, 1), key=lambda s: (topo.may_write(me, nbr[s]), topo.mates(topo.chip(me), topo.chip(nbr[s]))))
     calls = []
     for s in order:
@@ -78,7 +77,7 @@ def routes(T, topo, r):
         ef = bits(topo.mask(me, far[s]))[0::2]
         en = [e for e in bits(topo.mask(me, d if via is None else via)) if e not in ef]
         calls.append([dict(side=s, part=1, dst=d, via=far[s], eng=ef), dict(side=s, part=0, dst=d, via=via, eng=en)])
-    return calls
+    return calls, [near[order[1]], far[order[1]]]
 
 
 def landing(t):
@@ -99,12 +98,12 @@ def counter(q, sem):
     return step, settle
 
 
-def helper_program(g, core, T, topo):
+def relay_program(g, core, T, topo):
     for r in range(len(T.cores)):
-        near, far = helpers(T, topo, r)
-        if core in near + far:
-            invert(g, core, T, topo, T.cores[r], (near + far).index(core), neighbours(T, r))
-        for call in routes(T, topo, r):
+        calls, helping = plan(T, topo, r)
+        if core in helping:
+            invert(g, core, T, topo, T.cores[r], helping.index(core), neighbours(T, r))
+        for call in calls:
             for t in call:
                 if t["via"] != core:
                     continue
@@ -112,9 +111,9 @@ def helper_program(g, core, T, topo):
                 rid, pid, _ = topo.addr(t["dst"])
                 a, b = landing(t)
                 g.wait_ge(T.sem.rel, len(t["eng"]))
-                g.remote_dma(T.tab[:, a:b], T.relay[:], T.sem.arr, T.sem.sent0, pid, rid, m)
-                g.wait_ge(T.sem.sent0, len(bits(m)))
-        if core in near + far:
+                g.remote_dma(T.tab[:, a:b], T.relay[:], T.sem.arr, T.sem.sent, pid, rid, m)
+                g.wait_ge(T.sem.sent, len(bits(m)))
+        if core in helping:
             g.wait_ge(T.sem.isent, len(back_engines(topo, core, neighbours(T, r))))
 
 
@@ -122,20 +121,90 @@ def back_engines(topo, core, nbr):
     return bits(topo.mask(core, nbr[0]) & topo.mask(core, nbr[1]))
 
 
-def plc_engines(topo, me, cores, k):
-    return bits(topo.mask(me, cores[k]))[k::len(cores)]
+def plc_engines(topo, me, helper, k):
+    return bits(topo.mask(me, helper))[k::NH]
 
 
 def invert(g, core, T, topo, owner, k, nbr):
-    sem, v = T.sem, g.vector
-    step, settle = counter(v, sem.v)
-    flag = dict(allow_small_or_imprecise_dtypes=True)
+    sem, v, sc = T.sem, g.vector, g.scalar
     g.iota(T.pidx[:], [[1, 1]], 0, 1).then_inc(sem.gi, 1)
-    g.iota(T.qrow[:], [[0, 8], [1, 16]], 0, 0, **flag).then_inc(sem.gi, 1)
-    g.iota(T.ib[:], [[16, NB]], W, 0, **flag).then_inc(sem.gi, 1)
-    g.iota(T.crow[:], [[1, QC]], QC * k, 0, **flag).then_inc(sem.gi, 1)
-    g.iota(T.jrow[0:16, :], [[16, QC]], 16 * QC * k, 1, **flag).then_inc(sem.gi, 1)
-    v.wait_ge(sem.gi, 5)
+    g.iota(T.qrow[:], [[0, 8], [1, 16]], 0, 0, **FLAG).then_inc(sem.gi, 1)
+    g.iota(T.crow[:], [[1, QC]], QC * k, 0, **FLAG).then_inc(sem.gi, 1)
+    made = 3
+    for j, width in zip(STARTS, BLOCKS):
+        a, e = max(j // 16, QC * k) - QC * k, min((j + width) // 16, QC * (k + 1)) - QC * k
+        if a < e:
+            g.iota(T.jrow[0:16, a:e], [[16, e - a]], 16 * (QC * k + a) - j, 1, **FLAG).then_inc(sem.gi, 1)
+            made += 1
+    step, settle = counter(v, sem.v)
+    v.wait_ge(sem.gi, made)
+    step(v.tensor_copy(T.pf[:], T.pidx[:]))
+    settle()
+    step(v.tensor_scalar(T.rr[0:16, :], T.qrow[0:16, :], T.pf[0:16, :], None, AluOpType.is_equal))
+    settle()
+    v.wait_ge(sem.pl, len(plc_engines(topo, owner, core, k)))
+    sc.wait_ge(sem.gi, made)
+    sc.wait_ge(sem.pl, len(plc_engines(topo, owner, core, k)))
+    for b in range(VB, NB):
+        o = 128 * (b - VB)
+        sc.activation(T.ab[:, o:o + 128], T.qrow[:], ActivationFunctionType.Abs, bias=T.pv[:, b:b + 1],
+                      scale=-1.0).then_inc(sem.abr, 1)
+    sc.wait_ge(sem.abr, NB - VB)
+    for b in range(VB, NB):
+        o = 128 * (b - VB)
+        sc.activation(T.lq[:, 128 * b:128 * (b + 1)], T.ab[:, o:o + 128], ActivationFunctionType.Relu, bias=1.0,
+                      scale=-1.0).then_inc(sem["oh%d" % b], 1)
+    for b in range(NB):
+        s = sem["oh%d" % b]
+        if b < VB:
+            v.tensor_scalar(T.lq[:, 128 * b:128 * (b + 1)], T.qrow[:], T.pv[:, b:b + 1], None,
+                            AluOpType.is_equal).then_inc(s, 1)
+        v.tensor_scalar(T.rc[:, QC * b:QC * (b + 1)], T.crow[:], T.pv[:, NB + b:NB + b + 1],
+                        T.pv[:, 2 * NB + b:2 * NB + b + 1], AluOpType.is_equal, AluOpType.mult).then_inc(s, 1)
+    for b in range(NB):
+        g.tensor.wait_ge(sem["oh%d" % b], 2)
+        if b == 0:
+            g.tensor.matmul(T.ps_i[:, 0:QC], T.rr[0:16, :], T.jrow[0:16, :], True, False)
+        mm = g.tensor.matmul(T.ps_i[:, 0:QC], T.lq[:, 128 * b:128 * (b + 1)], T.rc[:, QC * b:QC * (b + 1)],
+                             False, b == NB - 1)
+    mm.then_inc(sem.t2, 1)
+    v.wait_ge(sem.t2, 1)
+    v.tensor_copy(T.part[:], T.ps_i[:, 0:QC]).then_inc(sem.partr, 1)
+    g.wait_ge(sem.partr, 1)
+    rid, pid, _ = topo.addr(owner)
+    g.remote_dma(T.inv[:, QC * k:QC * (k + 1)], T.part[:], sem.invr, sem.isent, pid, rid,
+                 mask_of(back_engines(topo, core, nbr)))
+
+
+def rank_program(g, core, T, topo):
+    rank = T.rank_of(core)
+    if rank is None:
+        relay_program(g, core, T, topo)
+        return
+    sem, v = T.sem, g.vector
+    calls, helping = plan(T, topo, rank)
+    arrivals = 0
+    for r in range(len(T.cores)):
+        for call in plan(T, topo, r)[0]:
+            for t in call:
+                if t["dst"] == core:
+                    arrivals += len(t["eng"]) if t["via"] is None else len(bits(topo.mask(t["via"], core)))
+    nsent = sum(len(t["eng"]) for call in calls for t in call)
+    ninv = sum(len(back_engines(topo, h, neighbours(T, rank))) for h in helping)
+
+    cut = STARTS[EARLY - 1]
+    g.sync.dma_start(T.sndi[0:16, :], T.snd[:]).then_inc(sem.lsnd, 16)
+    g.scalar.dma_start(T.plci[:], T.plc[:]).then_inc(sem.lplc, 16)
+    g.sync.dma_start(T.xs[:], T.x[:]).then_inc(sem.lx, 16)
+    g.sync.wait_ge(sem.ggo, 1)
+    g.sync.dma_start(T.tab[:, cut:W], T.gh[:, cut:W]).then_inc(sem.lga, 16)
+    g.sync.dma_start(T.tab[:, 0:cut], T.gh[:, 0:cut]).then_inc(sem.lgb, 16)
+
+    g.iota(T.pidx[:], [[1, 1]], 0, 1).then_inc(sem.gi, 1)
+    g.iota(T.ib[:], [[16, NB]], W, 0, **FLAG).then_inc(sem.gi, 1)
+    g.iota(T.qrow[0:16, :], [[0, 8], [1, 16]], 0, 0, **FLAG).then_inc(sem.gi, 1)
+    step, settle = counter(v, sem.v)
+    v.wait_ge(sem.gi, 3)
     step(v.tensor_scalar(T.mi[:], T.pidx[:], 7, None, AluOpType.bitwise_and))
     step(v.tensor_scalar(T.qi[:], T.pidx[:], 3, None, AluOpType.logical_shift_right))
     step(v.tensor_copy(T.pf[:], T.pidx[:]))
@@ -146,86 +215,22 @@ def invert(g, core, T, topo, owner, k, nbr):
     settle()
     step(v.tensor_scalar(T.iv[:], T.ib[:], T.mf[:], T.qf[:], AluOpType.add, AluOpType.add))
     settle()
-    v.wait_ge(sem.pl, len(plc_engines(topo, owner, [core] * NH, k)))
-    step(v.tensor_scalar(T.phi[:], T.plci[:], 4, None, AluOpType.logical_shift_right))
+    v.wait_ge(sem.lplc, 16)
     step(v.tensor_scalar(T.pli[:], T.plci[:], 15, None, AluOpType.bitwise_and))
+    step(v.tensor_scalar(T.phi[:], T.plci[:], 4, None, AluOpType.logical_shift_right))
     step(v.tensor_copy(T.plcf[:], T.plci[:]))
     settle()
-    step(v.tensor_copy(T.phf[:], T.phi[:]))
-    step(v.tensor_copy(T.plf[:], T.pli[:]))
-    step(v.tensor_tensor(T.val[:], T.iv[:], T.plcf[:], AluOpType.subtract))
-    settle()
-    for b in range(NB):
-        s = sem["oh%d" % b]
-        v.tensor_scalar(T.lq[:, 128 * b:128 * (b + 1)], T.qrow[:], T.plf[:, b:b + 1], None,
-                        AluOpType.is_equal).then_inc(s, 1)
-        v.tensor_scalar(T.rc[:, QC * b:QC * (b + 1)], T.crow[:], T.phf[:, b:b + 1], T.val[:, b:b + 1],
-                        AluOpType.is_equal, AluOpType.mult).then_inc(s, 1)
-    for b in range(NB):
-        g.tensor.wait_ge(sem["oh%d" % b], 2)
-        if b == 0:
-            g.tensor.matmul(T.ps_i[:, 0:QC], T.rr[0:16, :], T.jrow[0:16, :], True, False)
-        mm = g.tensor.matmul(T.ps_i[:, 0:QC], T.lq[:, 128 * b:128 * (b + 1)], T.rc[:, QC * b:QC * (b + 1)],
-                             False, b == NB - 1)
-    mm.then_inc(sem.t2, 1)
-    v.wait_ge(sem.t2, 1)
-    pieces = 0
-    for j, width in zip(STARTS, BLOCKS):
-        a, e = max(j // 16, QC * k) - QC * k, min((j + width) // 16, QC * (k + 1)) - QC * k
-        if a < e:
-            v.tensor_scalar(T.part[:, a:e], T.ps_i[:, a:e], j, None, AluOpType.subtract).then_inc(sem.partr, 1)
-            pieces += 1
-    g.wait_ge(sem.partr, pieces)
-    rid, pid, _ = topo.addr(owner)
-    g.remote_dma(T.inv[:, QC * k:QC * (k + 1)], T.part[:], sem.invr, sem.isent, pid, rid,
-                 mask_of(back_engines(topo, core, nbr)))
-
-
-def rank_program(g, core, T, topo):
-    rank = T.rank_of(core)
-    if rank is None:
-        helper_program(g, core, T, topo)
-        return
-    sem, v = T.sem, g.vector
-    calls = routes(T, topo, rank)
-    near, far = helpers(T, topo, rank)
-    help4 = near + far
-    arrivals = 0
-    for r in range(len(T.cores)):
-        for call in routes(T, topo, r):
-            for t in call:
-                if t["dst"] == core:
-                    arrivals += len(t["eng"]) if t["via"] is None else len(bits(topo.mask(t["via"], core)))
-    nsent = [sum(len(t["eng"]) for t in call) for call in calls]
-    ninv = sum(len(back_engines(topo, h, neighbours(T, rank))) for h in help4)
-
-    cut = STARTS[EARLY - 1]
-    g.sync.dma_start(T.sndi[0:16, :], T.snd[:]).then_inc(sem.lsnd, 16)
-    g.scalar.dma_start(T.plci[:], T.plc[:]).then_inc(sem.lplc, 16)
-    g.sync.dma_start(T.xs[:], T.x[:]).then_inc(sem.lx, 16)
-    g.sync.wait_ge(sem.pgo, 1)
-    g.sync.wait_ge(sem.ofsr, 1)
-    g.sync.dma_start(T.tab[:, cut:W], T.gh[:, cut:W]).then_inc(sem.lga, 16)
-    g.sync.wait_ge(sem.sent0, nsent[0])
-    g.sync.dma_start(T.tab[:, 0:cut], T.gh[:, 0:cut]).then_inc(sem.lgb, 16)
-
-    g.iota(T.pidx[:], [[1, 1]], 0, 1).then_inc(sem.gi, 1)
-    g.iota(T.qrow[:], [[0, 8], [1, 16]], 0, 0, allow_small_or_imprecise_dtypes=True).then_inc(sem.gi, 1)
-    g.wait_ge(sem.lplc, 16)
+    v.tensor_copy(T.pv[:, 0:NB], T.pli[:]).then_inc(sem.pvr, 1)
+    v.tensor_copy(T.pv[:, NB:2 * NB], T.phi[:]).then_inc(sem.pvr, 1)
+    v.tensor_tensor(T.pv[:, 2 * NB:3 * NB], T.iv[:], T.plcf[:], AluOpType.subtract).then_inc(sem.pvr, 1)
+    g.wait_ge(sem.pvr, 3)
     transfers = []
-    for k, h in enumerate(help4):
+    for k, h in enumerate(helping):
         rid, pid, _ = topo.addr(h)
-        transfers.append(RemoteDMATransfer(dst_ids=[DstId(rid=rid, pnc=pid)], remote_sem=sem.pl, src=T.plci[:], dst=T.plci[:],
-                                           dma_engine_mask=mask_of(plc_engines(topo, core, help4, k))))
+        transfers.append(RemoteDMATransfer(dst_ids=[DstId(rid=rid, pnc=pid)], remote_sem=sem.pl, src=T.pv[:], dst=T.pv[:],
+                                           dma_engine_mask=mask_of(plc_engines(topo, core, h, k))))
     g.remote_dma_fused(transfers, local_sem=sem.psent)
-    g.sem_inc(sem.pgo, 1)
 
-    step, settle = counter(v, sem.v)
-    v.wait_ge(sem.gi, 2)
-    step(v.tensor_copy(T.pf[:], T.pidx[:]))
-    settle()
-    step(v.tensor_scalar(T.rr[0:16, :], T.qrow[0:16, :], T.pf[0:16, :], None, AluOpType.is_equal))
-    settle()
     v.wait_ge(sem.lsnd, 16)
     v.tensor_copy(T.sndf[0:16, :], T.sndi[0:16, :]).then_inc(sem.sndr, 1)
     g.tensor.wait_ge(sem.sndr, 1)
@@ -254,10 +259,10 @@ def rank_program(g, core, T, topo):
             rid, pid, _ = topo.addr(to)
             transfers.append(RemoteDMATransfer(dst_ids=[DstId(rid=rid, pnc=pid)], dma_engine_mask=mask_of(t["eng"]),
                                                remote_sem=rs, src=src, dst=dst))
-        g.remote_dma_fused(transfers, local_sem=sem["sent%d" % k])
-    for k in range(len(calls)):
-        g.wait_ge(sem["sent%d" % k], nsent[k])
-    g.wait_ge(sem.psent, sum(len(plc_engines(topo, core, help4, k)) for k in range(NH)))
+        g.remote_dma_fused(transfers, local_sem=sem.sent)
+    g.sem_inc(sem.ggo, 1)
+    g.wait_ge(sem.sent, nsent)
+    g.wait_ge(sem.psent, sum(len(plc_engines(topo, core, h, k)) for k, h in enumerate(helping)))
 
     for q in (v, g.scalar):
         q.wait_ge(sem.invr, ninv)

@@ -5,11 +5,15 @@ SIM = 96
 W, CAP, HALF = 4096, 512, 256
 NB = 8
 VB = 5
-NH = 2
-QC = 256 // NH
-BLOCKS = (640, 1024, 1280, 1152)
+BLOCKS = (512, 1024, 1280, 1280)
 STARTS = [W - sum(BLOCKS[:_k + 1]) for _k in range(len(BLOCKS))]
 EARLY = 2
+CUT = STARTS[EARLY - 1] // 16
+NE = W // 16 - CUT
+NR = 4
+NT = NE // NR
+KQ, KC, KH, KL = 0, 16, 32, 48
+PV = KL + NB
 
 SCRATCH = {
     "xs": ("sbuf", [128, W], "float32"),
@@ -20,29 +24,35 @@ SCRATCH = {
     "sndi": ("sbuf", [128, 64], "int32"),
     "sndf": ("sbuf", [128, 64], "float32"),
     "ofs": ("sbuf", [128, 64], "uint16"),
-    "qrow": ("sbuf", [128, 128], "float32"),
+    "qrow": ("sbuf", [128, 128], "bfloat16"),
     "rr": ("sbuf", [128, 128], "float32"),
-    "crow": ("sbuf", [128, QC], "float32"),
-    "jrow": ("sbuf", [128, QC], "float32"),
-    "lq": ("sbuf", [128, NB * 128], "float32"),
-    "ab": ("sbuf", [128, (NB - VB) * 128], "float32"),
-    "rc": ("sbuf", [128, NB * QC], "float32"),
-    "part": ("sbuf", [128, QC], "uint16"),
-    "inv": ("sbuf", [128, NH * QC], "uint16"),
-    "pv": ("sbuf", [128, 3 * NB], "float32"),
+    "rrb": ("sbuf", [128, 128], "bfloat16"),
+    "qv": ("sbuf", [128, 4 * 128], "float32"),
+    "pv": ("sbuf", [128, PV], "float32"),
+    "npv": ("sbuf", [128, PV - KH], "float32"),
+    "crow": ("sbuf", [128, 256], "bfloat16"),
+    "hrow": ("sbuf", [128, 256], "bfloat16"),
+    "lqh": ("sbuf", [128, NB * 128], "bfloat16"),
+    "lql": ("sbuf", [128, NB * 128], "bfloat16"),
+    "ab": ("sbuf", [128, NB * 128], "bfloat16"),
+    "rc": ("sbuf", [128, NB * 256], "bfloat16"),
+    "quarter": ("sbuf", [128, NT], "bfloat16"),
+    "inve": ("sbuf", [128, NE], "uint16"),
+    "part": ("sbuf", [128, CUT], "uint16"),
+    "invl": ("sbuf", [128, CUT], "uint16"),
     "ps_s": ("psum", [128, 512], "float32"),
+    "ps_p": ("psum", [128, 512], "float32"),
     "ps_i": ("psum", [128, 512], "float32"),
 }
-for _name in ("plci", "phi", "pli"):
-    SCRATCH[_name] = ("sbuf", [128, NB], "int32")
-for _name in ("plcf", "ib", "iv"):
-    SCRATCH[_name] = ("sbuf", [128, NB], "float32")
-for _name in ("pidx", "mi", "qi"):
+for _name in ("plci", "ib", "qi", "ci", "di", "li"):
+    SCRATCH[_name] = ("sbuf", [128, 128], "int32")
+for _name in ("pidx", "mi"):
     SCRATCH[_name] = ("sbuf", [128, 1], "int32")
-for _name in ("pf", "mf", "qf"):
+for _name in ("pf", "mf"):
     SCRATCH[_name] = ("sbuf", [128, 1], "float32")
-SEMAPHORES = (["gi", "v", "lsnd", "lplc", "lx", "lga", "lgb", "sndr", "t1", "ofsr", "t2", "pl", "pvr", "abr", "ggo",
-               "psent", "partr", "isent", "invr", "g0", "g1", "rel", "sent", "arr", "st"]
+SEMAPHORES = (["gia", "gib", "gic", "v", "lsnd", "lplc", "lx", "lg0", "lg1", "lg2", "sndr", "t1", "ofsr", "qvr", "t3", "pvr",
+               "npr", "pl", "pvi", "abr", "ggo", "t2", "tabr", "tsent", "psent", "partr", "isent", "invr", "inver", "g0", "g1",
+               "rel", "sent", "arr", "st"]
               + ["oh%d" % b for b in range(NB)] + ["yr%d" % k for k in range(len(BLOCKS))])
 FLAG = dict(allow_small_or_imprecise_dtypes=True)
 
@@ -63,12 +73,21 @@ def neighbours(T, r):
     return [T.cores[(r - 1) % n], T.cores[(r + 1) % n]]
 
 
+def crew(T, topo, r):
+    me = T.cores[r]
+    nbr = neighbours(T, r)
+    chip = [c for c in range(SIM) if c != me and topo.chip(c) == topo.chip(me)]
+    own = [c for c in chip if all(topo.may_write(c, d) for d in nbr)]
+    near = [c for c in own if topo.die(c) == topo.die(me)][:2]
+    far = [c for c in own if topo.die(c) != topo.die(me)][:2]
+    rest = sorted((c for c in chip if c not in own), key=lambda c: topo.die(c) != topo.die(me))
+    return near, far, rest[0]
+
+
 def plan(T, topo, r):
     me = T.cores[r]
     nbr = neighbours(T, r)
-    own = [c for c in range(SIM) if c != me and topo.chip(c) == topo.chip(me) and all(topo.may_write(c, d) for d in nbr)]
-    near = [c for c in own if topo.die(c) == topo.die(me)]
-    far = [c for c in own if topo.die(c) != topo.die(me)]
+    near, far, _ = crew(T, topo, r)
     order = sorted((0, 1), key=lambda s: (topo.may_write(me, nbr[s]), topo.mates(topo.chip(me), topo.chip(nbr[s]))))
     calls = []
     for s in order:
@@ -77,12 +96,20 @@ def plan(T, topo, r):
         ef = bits(topo.mask(me, far[s]))[0::2]
         en = [e for e in bits(topo.mask(me, d if via is None else via)) if e not in ef]
         calls.append([dict(side=s, part=1, dst=d, via=far[s], eng=ef), dict(side=s, part=0, dst=d, via=via, eng=en)])
-    return calls, [near[order[1]], far[order[1]]]
+    return calls
 
 
 def landing(t):
     a = W + (CAP if t["side"] == 0 else 0) + t["part"] * HALF
     return a, a + HALF
+
+
+def off_engines(topo, core, nbr):
+    return bits(topo.mask(core, nbr[0]) & topo.mask(core, nbr[1]))
+
+
+def back_engines(topo, helper, me):
+    return bits(topo.mask(helper, me))[0::2]
 
 
 def counter(q, sem):
@@ -98,145 +125,176 @@ def counter(q, sem):
     return step, settle
 
 
-def relay_program(g, core, T, topo):
+def other_program(g, core, T, topo):
     for r in range(len(T.cores)):
-        calls, helping = plan(T, topo, r)
-        if core in helping:
-            invert(g, core, T, topo, T.cores[r], helping.index(core), neighbours(T, r))
-        for call in calls:
-            for t in call:
-                if t["via"] != core:
-                    continue
-                m = topo.mask(core, t["dst"])
-                rid, pid, _ = topo.addr(t["dst"])
-                a, b = landing(t)
-                g.wait_ge(T.sem.rel, len(t["eng"]))
-                g.remote_dma(T.tab[:, a:b], T.relay[:], T.sem.arr, T.sem.sent, pid, rid, m)
-                g.wait_ge(T.sem.sent, len(bits(m)))
-        if core in helping:
-            g.wait_ge(T.sem.isent, len(back_engines(topo, core, neighbours(T, r))))
+        near, far, helper = crew(T, topo, r)
+        me, nbr = T.cores[r], neighbours(T, r)
+        rid, pid, _ = topo.addr(me)
+        if core == helper:
+            help_program(g, core, T, topo, me)
+        relays = near + far
+        if core in relays:
+            k = relays.index(core)
+            eng = off_engines(topo, core, nbr)
+            g.iota(T.quarter[:], [[1, NT]], CUT + NT * k, 0, **FLAG).then_inc(T.sem.gia, 1)
+            g.wait_ge(T.sem.gia, 1)
+            g.remote_dma(T.crow[:, NT * k:NT * (k + 1)], T.quarter[:], T.sem.tabr, T.sem.tsent, pid, rid, mask_of(eng))
+            for call in plan(T, topo, r):
+                for t in call:
+                    if t["via"] != core:
+                        continue
+                    m = topo.mask(core, t["dst"])
+                    drid, dpid, _ = topo.addr(t["dst"])
+                    a, b = landing(t)
+                    g.wait_ge(T.sem.rel, len(t["eng"]))
+                    g.remote_dma(T.tab[:, a:b], T.relay[:], T.sem.arr, T.sem.sent, dpid, drid, m)
+                    g.wait_ge(T.sem.sent, len(bits(m)))
+            g.wait_ge(T.sem.tsent, len(eng))
 
 
-def back_engines(topo, core, nbr):
-    return bits(topo.mask(core, nbr[0]) & topo.mask(core, nbr[1]))
-
-
-def plc_engines(topo, me, helper, k):
-    return bits(topo.mask(me, helper))[k::NH]
-
-
-def invert(g, core, T, topo, owner, k, nbr):
-    sem, v, sc = T.sem, g.vector, g.scalar
-    g.iota(T.pidx[:], [[1, 1]], 0, 1).then_inc(sem.gi, 1)
-    g.iota(T.qrow[:], [[0, 8], [1, 16]], 0, 0, **FLAG).then_inc(sem.gi, 1)
-    g.iota(T.crow[:], [[1, QC]], QC * k, 0, **FLAG).then_inc(sem.gi, 1)
-    made = 3
+def base_rows(g, T, c0, n):
+    made = 0
     for j, width in zip(STARTS, BLOCKS):
-        a, e = max(j // 16, QC * k) - QC * k, min((j + width) // 16, QC * (k + 1)) - QC * k
+        a, e = max(j // 16, c0) - c0, min((j + width) // 16, c0 + n) - c0
         if a < e:
-            g.iota(T.jrow[0:16, a:e], [[16, e - a]], 16 * (QC * k + a) - j, 1, **FLAG).then_inc(sem.gi, 1)
+            g.iota(T.hrow[0:16, a:e], [[16, e - a]], 16 * (c0 + a) - j, 0, **FLAG).then_inc(T.sem.gic, 1)
             made += 1
-    step, settle = counter(v, sem.v)
-    v.wait_ge(sem.gi, made)
+    return made
+
+
+def constants(g, T, step, settle):
+    v = g.vector
+    v.wait_ge(T.sem.gia, 2)
     step(v.tensor_copy(T.pf[:], T.pidx[:]))
+    step(v.tensor_scalar(T.mi[:], T.pidx[:], 15, None, AluOpType.bitwise_and))
     settle()
-    step(v.tensor_scalar(T.rr[0:16, :], T.qrow[0:16, :], T.pf[0:16, :], None, AluOpType.is_equal))
-    settle()
-    v.wait_ge(sem.pl, len(plc_engines(topo, owner, core, k)))
-    sc.wait_ge(sem.gi, made)
-    sc.wait_ge(sem.pl, len(plc_engines(topo, owner, core, k)))
+    step(v.tensor_scalar(T.rrb[0:16, :], T.qrow[0:16, :], T.pf[0:16, :], None, AluOpType.is_equal))
+    step(v.tensor_copy(T.mf[:], T.mi[:]))
+
+
+def inversion(g, T, n, made, out, done, table=None):
+    sem, v, sc = T.sem, g.vector, g.scalar
+    sc.wait_ge(sem.npr, 1)
     for b in range(VB, NB):
-        o = 128 * (b - VB)
-        sc.activation(T.ab[:, o:o + 128], T.qrow[:], ActivationFunctionType.Abs, bias=T.pv[:, b:b + 1],
+        sc.activation(T.ab[:, 128 * b:128 * (b + 1)], T.qrow[:], ActivationFunctionType.Abs, bias=T.pv[:, KQ + b:KQ + b + 1],
                       scale=-1.0).then_inc(sem.abr, 1)
     sc.wait_ge(sem.abr, NB - VB)
     for b in range(VB, NB):
-        o = 128 * (b - VB)
-        sc.activation(T.lq[:, 128 * b:128 * (b + 1)], T.ab[:, o:o + 128], ActivationFunctionType.Relu, bias=1.0,
-                      scale=-1.0).then_inc(sem["oh%d" % b], 1)
+        for dst, k in ((T.lqh, KH), (T.lql, KL)):
+            sc.activation(dst[:, 128 * b:128 * (b + 1)], T.ab[:, 128 * b:128 * (b + 1)], ActivationFunctionType.Relu,
+                          bias=T.pv[:, k + b:k + b + 1],
+                          scale=T.npv[:, k - KH + b:k - KH + b + 1]).then_inc(sem["oh%d" % b], 1)
+    if table is not None:
+        v.wait_ge(sem.tabr, table)
     for b in range(NB):
         s = sem["oh%d" % b]
         if b < VB:
-            v.tensor_scalar(T.lq[:, 128 * b:128 * (b + 1)], T.qrow[:], T.pv[:, b:b + 1], None,
-                            AluOpType.is_equal).then_inc(s, 1)
-        v.tensor_scalar(T.rc[:, QC * b:QC * (b + 1)], T.crow[:], T.pv[:, NB + b:NB + b + 1],
-                        T.pv[:, 2 * NB + b:2 * NB + b + 1], AluOpType.is_equal, AluOpType.mult).then_inc(s, 1)
+            for dst, k in ((T.lqh, KH), (T.lql, KL)):
+                v.tensor_scalar(dst[:, 128 * b:128 * (b + 1)], T.qrow[:], T.pv[:, KQ + b:KQ + b + 1],
+                                T.pv[:, k + b:k + b + 1], AluOpType.is_equal, AluOpType.mult).then_inc(s, 1)
+        v.tensor_scalar(T.rc[:, n * b:n * (b + 1)], T.crow[:, 0:n], T.pv[:, KC + b:KC + b + 1], None,
+                        AluOpType.is_equal).then_inc(s, 1)
+    g.tensor.wait_ge(sem.gic, made)
     for b in range(NB):
-        g.tensor.wait_ge(sem["oh%d" % b], 2)
+        g.tensor.wait_ge(sem["oh%d" % b], 3)
         if b == 0:
-            g.tensor.matmul(T.ps_i[:, 0:QC], T.rr[0:16, :], T.jrow[0:16, :], True, False)
-        mm = g.tensor.matmul(T.ps_i[:, 0:QC], T.lq[:, 128 * b:128 * (b + 1)], T.rc[:, QC * b:QC * (b + 1)],
-                             False, b == NB - 1)
+            g.tensor.matmul(T.ps_i[:, 0:n], T.rrb[0:16, :], T.hrow[0:16, 0:n], True, False)
+        g.tensor.matmul(T.ps_i[:, 0:n], T.lqh[:, 128 * b:128 * (b + 1)], T.rc[:, n * b:n * (b + 1)], False, False)
+        mm = g.tensor.matmul(T.ps_i[:, 0:n], T.lql[:, 128 * b:128 * (b + 1)], T.rc[:, n * b:n * (b + 1)], False, b == NB - 1)
     mm.then_inc(sem.t2, 1)
     v.wait_ge(sem.t2, 1)
-    v.tensor_copy(T.part[:], T.ps_i[:, 0:QC]).then_inc(sem.partr, 1)
+    v.tensor_scalar(out[:], T.ps_i[:, 0:n], T.mf[:], None, AluOpType.add).then_inc(done, 1)
+
+
+def help_program(g, core, T, topo, me):
+    sem, v = T.sem, g.vector
+    g.iota(T.pidx[:], [[1, 1]], 0, 1).then_inc(sem.gia, 1)
+    g.iota(T.qrow[:], [[0, 8], [1, 16]], 0, 0, **FLAG).then_inc(sem.gia, 1)
+    g.iota(T.crow[:, 0:CUT], [[1, CUT]], 0, 0, **FLAG).then_inc(sem.gib, 1)
+    made = base_rows(g, T, 0, CUT)
+    step, settle = counter(v, sem.v)
+    constants(g, T, step, settle)
+    settle()
+    v.wait_ge(sem.gib, 1)
+    v.wait_ge(sem.pl, len(bits(topo.mask(me, core))))
+    v.tensor_scalar(T.npv[:], T.pv[:, KH:PV], -1, None, AluOpType.mult).then_inc(sem.npr, 1)
+    inversion(g, T, CUT, made, T.part, sem.partr)
     g.wait_ge(sem.partr, 1)
-    rid, pid, _ = topo.addr(owner)
-    g.remote_dma(T.inv[:, QC * k:QC * (k + 1)], T.part[:], sem.invr, sem.isent, pid, rid,
-                 mask_of(back_engines(topo, core, nbr)))
+    rid, pid, _ = topo.addr(me)
+    eng = back_engines(topo, core, me)
+    g.remote_dma(T.invl[:], T.part[:], sem.invr, sem.isent, pid, rid, mask_of(eng))
+    g.wait_ge(sem.isent, len(eng))
 
 
 def rank_program(g, core, T, topo):
     rank = T.rank_of(core)
     if rank is None:
-        relay_program(g, core, T, topo)
+        other_program(g, core, T, topo)
         return
     sem, v = T.sem, g.vector
-    calls, helping = plan(T, topo, rank)
+    near, far, helper = crew(T, topo, rank)
+    calls = plan(T, topo, rank)
     arrivals = 0
     for r in range(len(T.cores)):
-        for call in plan(T, topo, r)[0]:
+        for call in plan(T, topo, r):
             for t in call:
                 if t["dst"] == core:
                     arrivals += len(t["eng"]) if t["via"] is None else len(bits(topo.mask(t["via"], core)))
     nsent = sum(len(t["eng"]) for call in calls for t in call)
-    ninv = sum(len(back_engines(topo, h, neighbours(T, rank))) for h in helping)
+    ntab = sum(len(off_engines(topo, c, neighbours(T, rank))) for c in near + far)
+    hmask = topo.mask(core, helper)
 
-    cut = STARTS[EARLY - 1]
     g.sync.dma_start(T.sndi[0:16, :], T.snd[:]).then_inc(sem.lsnd, 16)
-    g.scalar.dma_start(T.plci[:], T.plc[:]).then_inc(sem.lplc, 16)
+    g.scalar.dma_start(T.plci[0:16, 0:64], T.plc[:]).then_inc(sem.lplc, 16)
     g.sync.dma_start(T.xs[:], T.x[:]).then_inc(sem.lx, 16)
+    g.sync.wait_ge(sem.pvi, 1)
+    g.sync.dma_start(T.tab[:, STARTS[0]:W], T.gh[:, STARTS[0]:W]).then_inc(sem.lg0, 16)
     g.sync.wait_ge(sem.ggo, 1)
-    g.sync.dma_start(T.tab[:, cut:W], T.gh[:, cut:W]).then_inc(sem.lga, 16)
-    g.sync.dma_start(T.tab[:, 0:cut], T.gh[:, 0:cut]).then_inc(sem.lgb, 16)
+    g.sync.dma_start(T.tab[:, STARTS[1]:STARTS[0]], T.gh[:, STARTS[1]:STARTS[0]]).then_inc(sem.lg1, 16)
+    g.sync.dma_start(T.tab[:, 0:STARTS[1]], T.gh[:, 0:STARTS[1]]).then_inc(sem.lg2, 16)
 
-    g.iota(T.pidx[:], [[1, 1]], 0, 1).then_inc(sem.gi, 1)
-    g.iota(T.ib[:], [[16, NB]], W, 0, **FLAG).then_inc(sem.gi, 1)
-    g.iota(T.qrow[0:16, :], [[0, 8], [1, 16]], 0, 0, **FLAG).then_inc(sem.gi, 1)
+    g.iota(T.pidx[:], [[1, 1]], 0, 1).then_inc(sem.gia, 1)
+    g.iota(T.qrow[:], [[0, 8], [1, 16]], 0, 0, **FLAG).then_inc(sem.gia, 1)
+    g.iota(T.ib[0:16, :], [[0, 2], [16, 64]], W, 1).then_inc(sem.gib, 1)
+    made = base_rows(g, T, CUT, NE)
     step, settle = counter(v, sem.v)
-    v.wait_ge(sem.gi, 3)
-    step(v.tensor_scalar(T.mi[:], T.pidx[:], 7, None, AluOpType.bitwise_and))
-    step(v.tensor_scalar(T.qi[:], T.pidx[:], 3, None, AluOpType.logical_shift_right))
-    step(v.tensor_copy(T.pf[:], T.pidx[:]))
-    settle()
-    step(v.tensor_scalar(T.mf[:], T.mi[:], 128, None, AluOpType.mult))
-    step(v.tensor_copy(T.qf[:], T.qi[:]))
+    constants(g, T, step, settle)
     step(v.tensor_scalar(T.rr[0:16, :], T.qrow[0:16, :], T.pf[0:16, :], None, AluOpType.is_equal))
     settle()
-    step(v.tensor_scalar(T.iv[:], T.ib[:], T.mf[:], T.qf[:], AluOpType.add, AluOpType.add))
-    settle()
-    v.wait_ge(sem.lplc, 16)
-    step(v.tensor_scalar(T.pli[:], T.plci[:], 15, None, AluOpType.bitwise_and))
-    step(v.tensor_scalar(T.phi[:], T.plci[:], 4, None, AluOpType.logical_shift_right))
-    step(v.tensor_copy(T.plcf[:], T.plci[:]))
-    settle()
-    v.tensor_copy(T.pv[:, 0:NB], T.pli[:]).then_inc(sem.pvr, 1)
-    v.tensor_copy(T.pv[:, NB:2 * NB], T.phi[:]).then_inc(sem.pvr, 1)
-    v.tensor_tensor(T.pv[:, 2 * NB:3 * NB], T.iv[:], T.plcf[:], AluOpType.subtract).then_inc(sem.pvr, 1)
-    g.wait_ge(sem.pvr, 3)
-    transfers = []
-    for k, h in enumerate(helping):
-        rid, pid, _ = topo.addr(h)
-        transfers.append(RemoteDMATransfer(dst_ids=[DstId(rid=rid, pnc=pid)], remote_sem=sem.pl, src=T.pv[:], dst=T.pv[:],
-                                           dma_engine_mask=mask_of(plc_engines(topo, core, h, k))))
-    g.remote_dma_fused(transfers, local_sem=sem.psent)
 
     v.wait_ge(sem.lsnd, 16)
     v.tensor_copy(T.sndf[0:16, :], T.sndi[0:16, :]).then_inc(sem.sndr, 1)
     g.tensor.wait_ge(sem.sndr, 1)
     g.tensor.matmul(T.ps_s[:, 0:64], T.rr[0:16, :], T.sndf[0:16, :], True, True).then_inc(sem.t1, 1)
+    v.wait_ge(sem.lplc, 16)
+    step(v.tensor_copy(T.plci[0:16, 64:128], T.plci[0:16, 0:64]))
+    settle()
+    v.wait_ge(sem.gib, 1)
+    step(v.tensor_scalar(T.qi[0:16, :], T.plci[0:16, :], 15, None, AluOpType.bitwise_and))
+    step(v.tensor_scalar(T.ci[0:16, :], T.plci[0:16, :], 4, None, AluOpType.logical_shift_right))
+    step(v.tensor_tensor(T.di[0:16, :], T.ib[0:16, :], T.plci[0:16, :], AluOpType.subtract))
+    settle()
+    step(v.tensor_scalar(T.li[0:16, :], T.di[0:16, :], 63, None, AluOpType.bitwise_and))
+    v.tensor_copy(T.qv[0:16, 0:128], T.qi[0:16, :]).then_inc(sem.qvr, 1)
+    v.tensor_copy(T.qv[0:16, 128:256], T.ci[0:16, :]).then_inc(sem.qvr, 1)
+    settle()
+    v.tensor_tensor(T.qv[0:16, 256:384], T.di[0:16, :], T.li[0:16, :], AluOpType.subtract).then_inc(sem.qvr, 1)
+    v.tensor_copy(T.qv[0:16, 384:512], T.li[0:16, :]).then_inc(sem.qvr, 1)
+    g.tensor.wait_ge(sem.qvr, 4)
+    for k in range(4):
+        g.tensor.matmul(T.ps_p[:, 16 * k:16 * (k + 1)], T.qv[0:16, 128 * k:128 * (k + 1)], T.rr[0:16, 0:16], True,
+                        True).then_inc(sem.t3, 1)
     v.wait_ge(sem.t1, 1)
     v.tensor_copy(T.ofs[:], T.ps_s[:, 0:64]).then_inc(sem.ofsr, 1)
+    v.wait_ge(sem.t3, 4)
+    v.tensor_copy(T.pv[0:64, :], T.ps_p[0:64, 0:PV]).then_inc(sem.pvr, 1)
+    v.tensor_copy(T.pv[64:128, :], T.ps_p[64:128, NB:NB + PV]).then_inc(sem.pvr, 1)
+    v.wait_ge(sem.pvr, 2)
+    v.tensor_scalar(T.npv[:], T.pv[:, KH:PV], -1, None, AluOpType.mult).then_inc(sem.npr, 1)
+    g.wait_ge(sem.pvr, 2)
+    rid, pid, _ = topo.addr(helper)
+    g.remote_dma(T.pv[:], T.pv[:], sem.pl, sem.psent, pid, rid, hmask)
+    g.sem_inc(sem.pvi, 1)
 
     for q in (v, g.scalar):
         q.wait_ge(sem.lx, 16)
@@ -262,22 +320,29 @@ def rank_program(g, core, T, topo):
         g.remote_dma_fused(transfers, local_sem=sem.sent)
     g.sem_inc(sem.ggo, 1)
     g.wait_ge(sem.sent, nsent)
-    g.wait_ge(sem.psent, sum(len(plc_engines(topo, core, h, k)) for k, h in enumerate(helping)))
+    g.wait_ge(sem.psent, len(bits(hmask)))
+
+    inversion(g, T, NE, made, T.inve, sem.inver, table=ntab)
 
     for q in (v, g.scalar):
-        q.wait_ge(sem.invr, ninv)
-        q.wait_ge(sem.lga, 16)
+        q.wait_ge(sem.inver, 1)
+        q.wait_ge(sem.lg0, 16)
         q.wait_ge(sem.arr, arrivals)
     for k, (j, width) in enumerate(zip(STARTS, BLOCKS)):
-        h = j + width // 2
         s = sem["yr%d" % k]
         win = T.tab[:, j:W + 2 * CAP]
-        if k == EARLY:
-            v.wait_ge(sem.lgb, 16)
-            g.scalar.wait_ge(sem.lgb, 16)
-        v.tensor_copy(T.ys[:, j:h], win.indirect(T.inv[:, j // 16:h // 16])).then_inc(s, 1)
-        g.scalar.activation(T.ys[:, h:j + width], win.indirect(T.inv[:, h // 16:(j + width) // 16]),
-                            ActivationFunctionType.Copy).then_inc(s, 1)
+        inv, o = (T.inve, CUT) if k < EARLY else (T.invl, 0)
+        a, m, b = j // 16 - o, (j + width // 2) // 16 - o, (j + width) // 16 - o
+        h = j + width // 2
+        for q in (v, g.scalar):
+            if k == 1:
+                q.wait_ge(sem.lg1, 16)
+            if k == 2:
+                q.wait_ge(sem.lg2, 16)
+            if k == EARLY:
+                q.wait_ge(sem.invr, len(back_engines(topo, helper, core)))
+        v.tensor_copy(T.ys[:, j:h], win.indirect(inv[:, a:m])).then_inc(s, 1)
+        g.scalar.activation(T.ys[:, h:j + width], win.indirect(inv[:, m:b]), ActivationFunctionType.Copy).then_inc(s, 1)
         g.sync.wait_ge(s, 2)
         g.sync.dma_start(T.y[:, j:j + width], T.ys[:, j:j + width]).then_inc(sem.st, 16)
     g.sync.wait_ge(sem.st, 16 * len(BLOCKS))

from concourse.bass import DstId, RemoteDMATransfer
from concourse.mybir import AluOpType, ActivationFunctionType

SIM = 96
W, CAP, HALF = 4096, 512, 256
NB = 8
VB = 5
BLOCKS = (512, 1024, 1280, 1280)
STARTS = [W - sum(BLOCKS[:_k + 1]) for _k in range(len(BLOCKS))]
EARLY = 2
CUT = STARTS[EARLY - 1] // 16
NE = W // 16 - CUT
NR = 4
NT = NE // NR
KQ, KC, KH, KL = 0, 16, 32, 48
PV = KL + NB

SCRATCH = {
    "xs": ("sbuf", [128, W], "float32"),
    "tab": ("sbuf", [128, W + 2 * CAP], "float32"),
    "ys": ("sbuf", [128, W], "float32"),
    "outb": ("sbuf", [128, 2 * CAP], "float32"),
    "relay": ("sbuf", [128, HALF], "float32"),
    "sndi": ("sbuf", [128, 64], "int32"),
    "sndf": ("sbuf", [128, 64], "float32"),
    "ofs": ("sbuf", [128, 64], "uint16"),
    "qrow": ("sbuf", [128, 128], "bfloat16"),
    "rr": ("sbuf", [128, 128], "float32"),
    "rrb": ("sbuf", [128, 128], "bfloat16"),
    "qv": ("sbuf", [128, 4 * 128], "float32"),
    "pv": ("sbuf", [128, PV], "float32"),
    "npv": ("sbuf", [128, PV - KH], "float32"),
    "crow": ("sbuf", [128, 256], "bfloat16"),
    "hrow": ("sbuf", [128, 256], "bfloat16"),
    "lqh": ("sbuf", [128, NB * 128], "bfloat16"),
    "lql": ("sbuf", [128, NB * 128], "bfloat16"),
    "ab": ("sbuf", [128, NB * 128], "bfloat16"),
    "rc": ("sbuf", [128, NB * 256], "bfloat16"),
    "quarter": ("sbuf", [128, NT], "bfloat16"),
    "inve": ("sbuf", [128, NE], "uint16"),
    "part": ("sbuf", [128, CUT], "uint16"),
    "invl": ("sbuf", [128, CUT], "uint16"),
    "ps_s": ("psum", [128, 512], "float32"),
    "ps_p": ("psum", [128, 512], "float32"),
    "ps_i": ("psum", [128, 512], "float32"),
}
for _name in ("plci", "ib", "qi", "ci", "di", "li"):
    SCRATCH[_name] = ("sbuf", [128, 128], "int32")
for _name in ("pidx", "mi"):
    SCRATCH[_name] = ("sbuf", [128, 1], "int32")
for _name in ("pf", "mf"):
    SCRATCH[_name] = ("sbuf", [128, 1], "float32")
SEMAPHORES = (["gia", "gib", "gic", "v", "lsnd", "lplc", "lx", "lg0", "lg1", "lg2", "sndr", "t1", "ofsr", "qvr", "t3", "pvr",
               "npr", "pl", "pvi", "abr", "ggo", "t2", "tabr", "tsent", "psent", "partr", "isent", "invr", "inver", "g0", "g1",
               "rel", "sent", "arr", "st"]
              + ["oh%d" % b for b in range(NB)] + ["yr%d" % k for k in range(len(BLOCKS))])
FLAG = dict(allow_small_or_imprecise_dtypes=True)


def bits(m):
    return [e for e in range(m.bit_length()) if (m >> e) & 1]


def mask_of(engines):
    m = 0
    for e in engines:
        m |= 1 << e
    return m


def neighbours(T, r):
    n = len(T.cores)
    return [T.cores[(r - 1) % n], T.cores[(r + 1) % n]]


def crew(T, topo, r):
    me = T.cores[r]
    nbr = neighbours(T, r)
    chip = [c for c in range(SIM) if c != me and topo.chip(c) == topo.chip(me)]
    own = [c for c in chip if all(topo.may_write(c, d) for d in nbr)]
    near = [c for c in own if topo.die(c) == topo.die(me)][:2]
    far = [c for c in own if topo.die(c) != topo.die(me)][:2]
    rest = sorted((c for c in chip if c not in own), key=lambda c: topo.die(c) != topo.die(me))
    return near, far, rest[0]


def plan(T, topo, r):
    me = T.cores[r]
    nbr = neighbours(T, r)
    near, far, _ = crew(T, topo, r)
    order = sorted((0, 1), key=lambda s: (topo.may_write(me, nbr[s]), topo.mates(topo.chip(me), topo.chip(nbr[s]))))
    calls = []
    for s in order:
        d = nbr[s]
        via = None if topo.may_write(me, d) else near[s]
        ef = bits(topo.mask(me, far[s]))[0::2]
        en = [e for e in bits(topo.mask(me, d if via is None else via)) if e not in ef]
        calls.append([dict(side=s, part=1, dst=d, via=far[s], eng=ef), dict(side=s, part=0, dst=d, via=via, eng=en)])
    return calls


def landing(t):
    a = W + (CAP if t["side"] == 0 else 0) + t["part"] * HALF
    return a, a + HALF


def off_engines(topo, core, nbr):
    return bits(topo.mask(core, nbr[0]) & topo.mask(core, nbr[1]))


def back_engines(topo, helper, me):
    return bits(topo.mask(helper, me))[0::2]


def counter(q, sem):
    n = [0]

    def step(call):
        call.then_inc(sem, 1)
        n[0] += 1

    def settle():
        q.wait_ge(sem, n[0])

    return step, settle


def other_program(g, core, T, topo):
    for r in range(len(T.cores)):
        near, far, helper = crew(T, topo, r)
        me, nbr = T.cores[r], neighbours(T, r)
        rid, pid, _ = topo.addr(me)
        if core == helper:
            help_program(g, core, T, topo, me)
        relays = near + far
        if core in relays:
            k = relays.index(core)
            eng = off_engines(topo, core, nbr)
            g.iota(T.quarter[:], [[1, NT]], CUT + NT * k, 0, **FLAG).then_inc(T.sem.gia, 1)
            g.wait_ge(T.sem.gia, 1)
            g.remote_dma(T.crow[:, NT * k:NT * (k + 1)], T.quarter[:], T.sem.tabr, T.sem.tsent, pid, rid, mask_of(eng))
            for call in plan(T, topo, r):
                for t in call:
                    if t["via"] != core:
                        continue
                    m = topo.mask(core, t["dst"])
                    drid, dpid, _ = topo.addr(t["dst"])
                    a, b = landing(t)
                    g.wait_ge(T.sem.rel, len(t["eng"]))
                    g.remote_dma(T.tab[:, a:b], T.relay[:], T.sem.arr, T.sem.sent, dpid, drid, m)
                    g.wait_ge(T.sem.sent, len(bits(m)))
            g.wait_ge(T.sem.tsent, len(eng))


def base_rows(g, T, c0, n):
    made = 0
    for j, width in zip(STARTS, BLOCKS):
        a, e = max(j // 16, c0) - c0, min((j + width) // 16, c0 + n) - c0
        if a < e:
            g.iota(T.hrow[0:16, a:e], [[16, e - a]], 16 * (c0 + a) - j, 0, **FLAG).then_inc(T.sem.gic, 1)
            made += 1
    return made


def constants(g, T, step, settle):
    v = g.vector
    v.wait_ge(T.sem.gia, 2)
    step(v.tensor_copy(T.pf[:], T.pidx[:]))
    step(v.tensor_scalar(T.mi[:], T.pidx[:], 15, None, AluOpType.bitwise_and))
    settle()
    step(v.tensor_scalar(T.rrb[0:16, :], T.qrow[0:16, :], T.pf[0:16, :], None, AluOpType.is_equal))
    step(v.tensor_copy(T.mf[:], T.mi[:]))


def inversion(g, T, n, made, out, done, table=None):
    sem, v, sc = T.sem, g.vector, g.scalar
    sc.wait_ge(sem.npr, 1)
    for b in range(VB, NB):
        sc.activation(T.ab[:, 128 * b:128 * (b + 1)], T.qrow[:], ActivationFunctionType.Abs, bias=T.pv[:, KQ + b:KQ + b + 1],
                      scale=-1.0).then_inc(sem.abr, 1)
    sc.wait_ge(sem.abr, NB - VB)
    for b in range(VB, NB):
        for dst, k in ((T.lqh, KH), (T.lql, KL)):
            sc.activation(dst[:, 128 * b:128 * (b + 1)], T.ab[:, 128 * b:128 * (b + 1)], ActivationFunctionType.Relu,
                          bias=T.pv[:, k + b:k + b + 1],
                          scale=T.npv[:, k - KH + b:k - KH + b + 1]).then_inc(sem["oh%d" % b], 1)
    if table is not None:
        v.wait_ge(sem.tabr, table)
    for b in range(NB):
        s = sem["oh%d" % b]
        if b < VB:
            for dst, k in ((T.lqh, KH), (T.lql, KL)):
                v.tensor_scalar(dst[:, 128 * b:128 * (b + 1)], T.qrow[:], T.pv[:, KQ + b:KQ + b + 1],
                                T.pv[:, k + b:k + b + 1], AluOpType.is_equal, AluOpType.mult).then_inc(s, 1)
        v.tensor_scalar(T.rc[:, n * b:n * (b + 1)], T.crow[:, 0:n], T.pv[:, KC + b:KC + b + 1], None,
                        AluOpType.is_equal).then_inc(s, 1)
    g.tensor.wait_ge(sem.gic, made)
    for b in range(NB):
        g.tensor.wait_ge(sem["oh%d" % b], 3)
        if b == 0:
            g.tensor.matmul(T.ps_i[:, 0:n], T.rrb[0:16, :], T.hrow[0:16, 0:n], True, False)
        g.tensor.matmul(T.ps_i[:, 0:n], T.lqh[:, 128 * b:128 * (b + 1)], T.rc[:, n * b:n * (b + 1)], False, False)
        mm = g.tensor.matmul(T.ps_i[:, 0:n], T.lql[:, 128 * b:128 * (b + 1)], T.rc[:, n * b:n * (b + 1)], False, b == NB - 1)
    mm.then_inc(sem.t2, 1)
    v.wait_ge(sem.t2, 1)
    v.tensor_scalar(out[:], T.ps_i[:, 0:n], T.mf[:], None, AluOpType.add).then_inc(done, 1)


def help_program(g, core, T, topo, me):
    sem, v = T.sem, g.vector
    g.iota(T.pidx[:], [[1, 1]], 0, 1).then_inc(sem.gia, 1)
    g.iota(T.qrow[:], [[0, 8], [1, 16]], 0, 0, **FLAG).then_inc(sem.gia, 1)
    g.iota(T.crow[:, 0:CUT], [[1, CUT]], 0, 0, **FLAG).then_inc(sem.gib, 1)
    made = base_rows(g, T, 0, CUT)
    step, settle = counter(v, sem.v)
    constants(g, T, step, settle)
    settle()
    v.wait_ge(sem.gib, 1)
    v.wait_ge(sem.pl, len(bits(topo.mask(me, core))))
    v.tensor_scalar(T.npv[:], T.pv[:, KH:PV], -1, None, AluOpType.mult).then_inc(sem.npr, 1)
    inversion(g, T, CUT, made, T.part, sem.partr)
    g.wait_ge(sem.partr, 1)
    rid, pid, _ = topo.addr(me)
    eng = back_engines(topo, core, me)
    g.remote_dma(T.invl[:], T.part[:], sem.invr, sem.isent, pid, rid, mask_of(eng))
    g.wait_ge(sem.isent, len(eng))


def rank_program(g, core, T, topo):
    rank = T.rank_of(core)
    if rank is None:
        other_program(g, core, T, topo)
        return
    sem, v = T.sem, g.vector
    near, far, helper = crew(T, topo, rank)
    calls = plan(T, topo, rank)
    arrivals = 0
    for r in range(len(T.cores)):
        for call in plan(T, topo, r):
            for t in call:
                if t["dst"] == core:
                    arrivals += len(t["eng"]) if t["via"] is None else len(bits(topo.mask(t["via"], core)))
    nsent = sum(len(t["eng"]) for call in calls for t in call)
    ntab = sum(len(off_engines(topo, c, neighbours(T, rank))) for c in near + far)
    hmask = topo.mask(core, helper)

    g.sync.dma_start(T.sndi[0:16, :], T.snd[:]).then_inc(sem.lsnd, 16)
    g.scalar.dma_start(T.plci[0:16, 0:64], T.plc[:]).then_inc(sem.lplc, 16)
    g.sync.dma_start(T.xs[:], T.x[:]).then_inc(sem.lx, 16)
    g.sync.wait_ge(sem.pvi, 1)
    g.sync.dma_start(T.tab[:, STARTS[0]:W], T.gh[:, STARTS[0]:W]).then_inc(sem.lg0, 16)
    g.sync.wait_ge(sem.ggo, 1)
    g.sync.dma_start(T.tab[:, STARTS[1]:STARTS[0]], T.gh[:, STARTS[1]:STARTS[0]]).then_inc(sem.lg1, 16)
    g.sync.dma_start(T.tab[:, 0:STARTS[1]], T.gh[:, 0:STARTS[1]]).then_inc(sem.lg2, 16)

    g.iota(T.pidx[:], [[1, 1]], 0, 1).then_inc(sem.gia, 1)
    g.iota(T.qrow[:], [[0, 8], [1, 16]], 0, 0, **FLAG).then_inc(sem.gia, 1)
    g.iota(T.ib[0:16, :], [[0, 2], [16, 64]], W, 1).then_inc(sem.gib, 1)
    made = base_rows(g, T, CUT, NE)
    step, settle = counter(v, sem.v)
    constants(g, T, step, settle)
    step(v.tensor_scalar(T.rr[0:16, :], T.qrow[0:16, :], T.pf[0:16, :], None, AluOpType.is_equal))
    settle()

    v.wait_ge(sem.lsnd, 16)
    v.tensor_copy(T.sndf[0:16, :], T.sndi[0:16, :]).then_inc(sem.sndr, 1)
    g.tensor.wait_ge(sem.sndr, 1)
    g.tensor.matmul(T.ps_s[:, 0:64], T.rr[0:16, :], T.sndf[0:16, :], True, True).then_inc(sem.t1, 1)
    v.wait_ge(sem.lplc, 16)
    step(v.tensor_copy(T.plci[0:16, 64:128], T.plci[0:16, 0:64]))
    settle()
    v.wait_ge(sem.gib, 1)
    step(v.tensor_scalar(T.qi[0:16, :], T.plci[0:16, :], 15, None, AluOpType.bitwise_and))
    step(v.tensor_scalar(T.ci[0:16, :], T.plci[0:16, :], 4, None, AluOpType.logical_shift_right))
    step(v.tensor_tensor(T.di[0:16, :], T.ib[0:16, :], T.plci[0:16, :], AluOpType.subtract))
    settle()
    step(v.tensor_scalar(T.li[0:16, :], T.di[0:16, :], 63, None, AluOpType.bitwise_and))
    v.tensor_copy(T.qv[0:16, 0:128], T.qi[0:16, :]).then_inc(sem.qvr, 1)
    v.tensor_copy(T.qv[0:16, 128:256], T.ci[0:16, :]).then_inc(sem.qvr, 1)
    settle()
    v.tensor_tensor(T.qv[0:16, 256:384], T.di[0:16, :], T.li[0:16, :], AluOpType.subtract).then_inc(sem.qvr, 1)
    v.tensor_copy(T.qv[0:16, 384:512], T.li[0:16, :]).then_inc(sem.qvr, 1)
    g.tensor.wait_ge(sem.qvr, 4)
    for k in range(4):
        g.tensor.matmul(T.ps_p[:, 16 * k:16 * (k + 1)], T.qv[0:16, 128 * k:128 * (k + 1)], T.rr[0:16, 0:16], True,
                        True).then_inc(sem.t3, 1)
    v.wait_ge(sem.t1, 1)
    v.tensor_copy(T.ofs[:], T.ps_s[:, 0:64]).then_inc(sem.ofsr, 1)
    v.wait_ge(sem.t3, 4)
    v.tensor_copy(T.pv[0:64, :], T.ps_p[0:64, 0:PV]).then_inc(sem.pvr, 1)
    v.tensor_copy(T.pv[64:128, :], T.ps_p[64:128, NB:NB + PV]).then_inc(sem.pvr, 1)
    v.wait_ge(sem.pvr, 2)
    v.tensor_scalar(T.npv[:], T.pv[:, KH:PV], -1, None, AluOpType.mult).then_inc(sem.npr, 1)
    g.wait_ge(sem.pvr, 2)
    rid, pid, _ = topo.addr(helper)
    g.remote_dma(T.pv[:], T.pv[:], sem.pl, sem.psent, pid, rid, hmask)
    g.sem_inc(sem.pvi, 1)

    for q in (v, g.scalar):
        q.wait_ge(sem.lx, 16)
        q.wait_ge(sem.ofsr, 1)
    for k, call in enumerate(calls):
        side = call[0]["side"]
        c, e = CAP * side, 32 * side
        v.tensor_copy(T.outb[:, c:c + HALF], T.xs[:].indirect(T.ofs[:, e:e + 16])).then_inc(sem["g%d" % k], 1)
        g.scalar.activation(T.outb[:, c + HALF:c + CAP], T.xs[:].indirect(T.ofs[:, e + 16:e + 32]),
                            ActivationFunctionType.Copy).then_inc(sem["g%d" % k], 1)
        g.wait_ge(sem["g%d" % k], 2)
        transfers = []
        for t in call:
            src = T.outb[:, c + t["part"] * HALF:c + (t["part"] + 1) * HALF]
            if t["via"] is None:
                a, b = landing(t)
                to, dst, rs = t["dst"], T.tab[:, a:b], sem.arr
            else:
                to, dst, rs = t["via"], T.relay[:], sem.rel
            rid, pid, _ = topo.addr(to)
            transfers.append(RemoteDMATransfer(dst_ids=[DstId(rid=rid, pnc=pid)], dma_engine_mask=mask_of(t["eng"]),
                                               remote_sem=rs, src=src, dst=dst))
        g.remote_dma_fused(transfers, local_sem=sem.sent)
    g.sem_inc(sem.ggo, 1)
    g.wait_ge(sem.sent, nsent)
    g.wait_ge(sem.psent, len(bits(hmask)))

    inversion(g, T, NE, made, T.inve, sem.inver, table=ntab)

    for q in (v, g.scalar):
        q.wait_ge(sem.inver, 1)
        q.wait_ge(sem.lg0, 16)
        q.wait_ge(sem.arr, arrivals)
    for k, (j, width) in enumerate(zip(STARTS, BLOCKS)):
        s = sem["yr%d" % k]
        win = T.tab[:, j:W + 2 * CAP]
        inv, o = (T.inve, CUT) if k < EARLY else (T.invl, 0)
        a, m, b = j // 16 - o, (j + width // 2) // 16 - o, (j + width) // 16 - o
        h = j + width // 2
        for q in (v, g.scalar):
            if k == 1:
                q.wait_ge(sem.lg1, 16)
            if k == 2:
                q.wait_ge(sem.lg2, 16)
            if k == EARLY:
                q.wait_ge(sem.invr, len(back_engines(topo, helper, core)))
        v.tensor_copy(T.ys[:, j:h], win.indirect(inv[:, a:m])).then_inc(s, 1)
        g.scalar.activation(T.ys[:, h:j + width], win.indirect(inv[:, m:b]), ActivationFunctionType.Copy).then_inc(s, 1)
        g.sync.wait_ge(s, 2)
        g.sync.dma_start(T.y[:, j:j + width], T.ys[:, j:j + width]).then_inc(sem.st, 16)
    g.sync.wait_ge(sem.st, 16 * len(BLOCKS))
